import numpy as np
import ml_dtypes


def mxq(x, axis, fmt="e4m3"):
    dtype, down = {"e4m3": (ml_dtypes.float8_e4m3fn, 7), "e5m2": (ml_dtypes.float8_e5m2, 14)}[fmt]
    v = np.moveaxis(np.asarray(x, np.float32).astype(ml_dtypes.bfloat16).astype(np.float64), axis, -1)
    blocks = v.reshape(v.shape[:-1] + (-1, 32))
    amax = np.abs(blocks).max(-1, keepdims=True)
    byte = np.maximum(np.where(amax > 0, np.frexp(amax)[1] - 1 + 127, 0) - down, 1)
    scale = np.exp2(byte - 127.0)
    codes = (blocks / scale).astype(np.float32).astype(dtype).astype(np.float64)
    return np.moveaxis((codes * scale).reshape(v.shape), -1, axis)


WIDE = False


def mx_kscale(k):
    if not WIDE:
        return np.ones(k)
    levels = np.array([10, -10, 5, -5, 0])
    if k % 512:
        return np.exp2(np.random.permutation(np.resize(levels, k // 32))).repeat(32)
    a = np.empty((k // 512, 16))
    for p in range(k // 512):
        a[p, :8] = np.random.permutation(np.resize(levels, 8))
        for g in range(8):
            far = levels[np.abs(levels - a[p, g]) >= 10]
            a[p, g + 8] = far[np.random.randint(len(far))]
    return np.exp2(a.ravel()).repeat(32)


def f64(x):
    return np.asarray(x).astype(np.float64)


def striped8(idx):
    return np.concatenate([x.reshape(-1, 16).T for x in idx]).astype(np.uint16)


def runs(offs, k):
    lists = np.stack([offs[16 * r : 16 * r + 16].T.reshape(-1) for r in range(8)]).astype(np.int64)
    return lists[np.arange(k) % 512 // 64]


def pack_weight(w):
    k, n = w.shape
    w = f64(np.asarray(w, np.float32).astype(ml_dtypes.bfloat16)).reshape(k // 32, 32, n)
    amax = np.abs(w).max(1)
    byte = np.clip(np.where(amax > 0, np.frexp(amax)[1] - 1 + 127 - 7, 1), 1, 254)
    scaled = (w * np.exp2(127.0 - byte)[:, None, :]).reshape(k, n).astype(np.float32)
    words = np.ascontiguousarray(scaled.reshape(k // 512, 128, 4, n).transpose(0, 1, 3, 2)).astype(ml_dtypes.float8_e4m3fn).view(np.uint8)
    return words, np.ascontiguousarray(byte.astype(np.uint8).reshape(k // 512, 16, n))


def unpack_weight(words, scales):
    g, p, n, _ = words.shape
    vals = np.ascontiguousarray(words).view(ml_dtypes.float8_e4m3fn).astype(np.float64) * np.repeat(np.exp2(scales.astype(np.float64) - 127.0), 8, axis=1)[..., None]
    return vals.transpose(0, 1, 3, 2).reshape(g * 512, n)


E2M1 = np.array([0.0, 0.5, 1.0, 1.5, 2.0, 3.0, 4.0, 6.0, -0.0, -0.5, -1.0, -1.5, -2.0, -3.0, -4.0, -6.0])


def pack_fp4(w):
    k, n = w.shape
    w = f64(np.asarray(w, np.float32).astype(ml_dtypes.bfloat16)).reshape(k // 32, 32, n)
    amax = np.abs(w).max(1)
    mant, ex = np.frexp(amax / 6.0)
    byte = np.clip(np.where(amax > 0, np.where(mant > 0.5, ex, ex - 1) + 127, 1), 1, 254)
    scaled = (w * np.exp2(127.0 - byte)[:, None, :]).reshape(k, n).astype(np.float32)
    c = np.ascontiguousarray(scaled.reshape(k // 512, 128, 4, n).transpose(0, 1, 3, 2)).astype(ml_dtypes.float4_e2m1fn).view(np.uint8) & 0xF
    words = (c[..., 0::2] | (c[..., 1::2] << 4)).reshape(k // 512, 128, 2 * n)
    return np.ascontiguousarray(words), np.ascontiguousarray(byte.astype(np.uint8).reshape(k // 512, 16, n))


def unpack_fp4(words, scales):
    g, _, n = scales.shape
    words = np.ascontiguousarray(words).reshape(g, 128, n, 2)
    nib = np.empty((g, 128, n, 4), np.uint8)
    nib[..., 0::2] = words & 0xF
    nib[..., 1::2] = words >> 4
    vals = E2M1[nib] * np.repeat(np.exp2(scales.astype(np.float64) - 127.0), 8, axis=1)[..., None]
    return vals.transpose(0, 1, 3, 2).reshape(g * 512, n)


def planes(y):
    n, m = y.shape
    v = y.astype(np.float32).astype(ml_dtypes.bfloat16).astype(np.float64).reshape(n // 32, 32, m)
    top = np.abs(v).max(1)
    byte = np.clip(np.where(top > 0, np.frexp(top)[1] - 1 + 127 - 7, 1), 1, 254)
    codes = (v * np.exp2(127.0 - byte)[:, None, :]).reshape(n, m).astype(np.float32).astype(ml_dtypes.float8_e4m3fn).view(np.uint8)
    words = codes.reshape(n // 512, 128, 4, m).transpose(0, 1, 3, 2)
    return np.ascontiguousarray(words), np.ascontiguousarray(byte.astype(np.uint8).reshape(n // 512, 16, m))


K, T, S, H = 512, 2048, 512, 512


def setup_inputs():
    n = np.random.standard_normal
    s = mx_kscale(K)[:, None]
    u = mx_kscale(H)
    packed_xT = pack_weight(n((K, T)) * s)
    packed_w1 = pack_fp4(n((K, H)) / np.sqrt(K) / s)
    packed_w2 = pack_fp4(n((H, H)) / np.sqrt(H) / u[:, None])
    return {
        "x_words": packed_xT[0],
        "x_scales": packed_xT[1],
        "w1_words": packed_w1[0],
        "w1_scales": packed_w1[1],
        "gn": (np.random.uniform(0.5, 1.5, (H, 1)) * u[:, None]).astype(np.float32),
        "dinv": np.random.uniform(0.3, 0.8, (H, S)).astype(np.float32),
        "w2_words": packed_w2[0],
        "w2_scales": packed_w2[1],
        "offs": striped8(np.stack([np.random.permutation(T)[:S] for _ in range(8)])),
        "nb": striped8(np.stack([np.random.permutation(S) for _ in range(8)])),
    }


def reference(x_words, x_scales, w1_words, w1_scales, gn, dinv, w2_words, w2_scales, offs, nb):
    xq = unpack_weight(x_words, x_scales)[np.arange(K)[:, None], runs(offs, K)]
    y = unpack_fp4(w1_words, w1_scales).T @ xq
    z = f64(gn) * y
    w2q = unpack_fp4(w2_words, w2_scales)
    x1 = f64(dinv) * (y - (0.5 * ((w2q.T @ mxq(z, 0, "e4m3")))))
    z2 = f64(gn) * (x1[np.arange(H)[:, None], runs(nb, H)])
    out_0 = f64(dinv) * (y - (0.5 * ((w2q.T @ mxq(z2, 0, "e4m3")))))
    return (out_0,) + planes(out_0)

@@ -1,0 +1,234 @@
+from contextlib import ExitStack
+
+import concourse.mybir as mybir
+
+F32 = mybir.dt.float32
+BF16 = mybir.dt.bfloat16
+I32 = mybir.dt.int32
+U32 = mybir.dt.uint32
+U16 = mybir.dt.uint16
+U8 = mybir.dt.uint8
+FP8X4 = mybir.dt.float8_e4m3fn_x4
+FP4X4 = mybir.dt.float4_e2m1fn_x4
+MULT = mybir.AluOpType.mult
+ADD = mybir.AluOpType.add
+
+P = 128
+PACK = 4
+T = 2048
+S = 512
+H = 512
+CHUNK = 128
+CHUNKS = S // CHUNK
+PER_COLUMN = 16
+FLOPS = 3 * 2 * 512 * 512 * 512
+
+
+def tile_picked_jacobi2_none_po_kernel(
+    tc, x_words, x_scales, w1_words, w1_scales, gn, dinv, w2_words, w2_scales, offs, nb, out_0, out_1, out_2
+):
+    nc = tc.nc
+    with ExitStack() as ctx:
+        lists = ctx.enter_context(tc.tile_pool(name="lists", bufs=1))
+        keep = ctx.enter_context(tc.tile_pool(name="keep", bufs=1))
+        psum = ctx.enter_context(tc.psum_pool(name="psum", bufs=1))
+
+        def cols(c):
+            return slice(c * CHUNK, (c + 1) * CHUNK)
+
+        def load_scale_rows(queue, scales, name):
+            raw = keep.tile([P, H], U8, name=name)
+            rows = scales[0].bitcast(I32)
+            for q in range(4):
+                queue.dma_start(
+                    out=raw[32 * q : 32 * q + 32, :].bitcast(I32),
+                    in_=rows[4 * q : 4 * q + 4, :].unsqueeze(0).to_broadcast([8, 4, H // 4]),
+                )
+            return raw
+
+        def deal(words_raw, scales_raw, name):
+            words = keep.tile([P, 2 * H], U8, name=name + "_words", align_bytes=64)
+            scales = keep.tile([P, H], U8, name=name + "_scales", align_bytes=64)
+            nc.vector.tensor_copy(
+                out=words[:].rearrange("p (t m b) -> p t m b", t=PACK, b=2),
+                in_=words_raw[:].rearrange("p (m t b) -> p t m b", t=PACK, b=2),
+            )
+            nc.vector.tensor_copy(
+                out=scales[:].rearrange("p (t m) -> p t m", t=PACK),
+                in_=scales_raw[:].rearrange("p (m t) -> p t m", t=PACK),
+            )
+            return words, scales
+
+        def product(bank, weights, t, codes, scales, start, stop):
+            words, wscales = weights
+            nc.tensor.matmul_mx(
+                out=bank,
+                lhsT=words[:, 2 * P * t : 2 * P * (t + 1)].bitcast(FP4X4),
+                lhsT_scale=wscales[:, P * t : P * (t + 1)],
+                rhs=codes.bitcast(FP8X4),
+                rhs_scale=scales,
+                start=start,
+                stop=stop,
+            )
+
+        def interleave(dst, src):
+            nc.scalar.copy(
+                out=dst.rearrange("p (c i) t -> p c t i", i=4),
+                in_=src.rearrange("p t (c i) -> p c t i", i=4),
+            )
+
+        def quantize(codes, scales, grouped):
+            nc.vector.quantize_mx(out=codes.bitcast(FP8X4), scales=scales, in_=grouped.rearrange("p n t -> p (n t)"))
+
+        offs_sb = lists.tile([P, S // PER_COLUMN], U16, name="offs_sb")
+        nb_sb = lists.tile([P, S // PER_COLUMN], U16, name="nb_sb")
+        xs_table = keep.tile([P, T], U8, name="xs_table")
+        xw_table = keep.tile([P, T], U32, name="xw_table")
+        w1_raw = keep.tile([P, 2 * H], U8, name="w1_raw")
+        w2_raw = keep.tile([P, 2 * H], U8, name="w2_raw")
+        gn_sb = keep.tile([P, PACK], F32, name="gn_sb")
+        xq_scales = keep.tile([P, S], U8, name="xq_scales", align_bytes=64)
+
+        nc.sync.dma_start(offs_sb[:], offs)
+        nc.sync.dma_start(
+            out=xs_table[:].bitcast(I32),
+            in_=x_scales[0].bitcast(I32).unsqueeze(1).to_broadcast([16, 8, T // 4]),
+        )
+        nc.scalar.dma_start(out=w1_raw[:].bitcast(I32), in_=w1_words[0].bitcast(I32))
+        w1s_raw = load_scale_rows(nc.scalar, w1_scales, "w1s_raw")
+        nc.sync.dma_start(
+            out=xw_table[:].bitcast(I32), in_=x_words[0].rearrange("p n t -> p (n t)").bitcast(I32)
+        )
+        nc.sync.dma_start(out=w2_raw[:].bitcast(I32), in_=w2_words[0].bitcast(I32))
+        nc.sync.dma_start(out=gn_sb[:], in_=gn.rearrange("(p t) o -> p (t o)", t=PACK))
+        nc.sync.dma_start(nb_sb[:], nb)
+        w2s_raw = keep.tile([P, H], U8, name="w2s_raw")
+        nc.vector.memset(w2s_raw[:].bitcast(I32), 0)
+        nc.vector.memset(xq_scales[:].bitcast(I32), 0)
+        for q in range(4):
+            nc.gpsimd.dma_start(
+                out=w2s_raw[32 * q : 32 * q + 4, :].bitcast(I32), in_=w2_scales[0].bitcast(I32)[4 * q : 4 * q + 4, :]
+            )
+
+        xs_picked = keep.tile([P, S], U8, name="xs_picked", tag="late")
+        nc.vector.tensor_copy(xs_picked[:], xs_table[:].indirect(offs_sb[:]))
+        for q in range(4):
+            nc.scalar.dma_start(
+                out=xq_scales[32 * q : 32 * q + 4, :].bitcast(I32),
+                in_=xs_picked[32 * q : 32 * q + 32 : 8, :].bitcast(I32),
+            )
+        dinv_sb = keep.tile([P, PACK, S], F32, name="dinv_sb", tag="late")
+        nc.sync.dma_start(out=dinv_sb[:], in_=dinv.rearrange("(p t) n -> p t n", t=PACK))
+
+        w1 = deal(w1_raw, w1s_raw, "w1")
+        xq_words = keep.tile([P, S], U32, name="xq_words", align_bytes=64)
+        half = S // 2
+        for h in range(2):
+            nc.vector.tensor_copy(
+                xq_words[:, h * half : (h + 1) * half],
+                xw_table[:].indirect(offs_sb[:, h * half // PER_COLUMN : (h + 1) * half // PER_COLUMN]),
+            )
+        w2 = deal(w2_raw, w2s_raw, "w2")
+        gn_half = keep.tile([P, PACK], F32, name="gn_half")
+        nc.vector.tensor_scalar(out=gn_half[:], in0=gn_sb[:], scalar1=-0.5, scalar2=None, op0=MULT)
+
+        y_sb = keep.tile([P, PACK, S], F32, name="y_sb")
+        z_codes = keep.tile([P, S], U32, name="z_codes", align_bytes=64)
+        z_scales = keep.tile([P, S], U8, name="z_scales", align_bytes=64)
+        sweep1 = [psum.tile([P, S], F32, name="sweep1_%d" % t) for t in range(PACK)]
+        y_banks = []
+        for c in range(CHUNKS):
+            bank = psum.tile([P, PACK, CHUNK], F32, name="y_bank", tag="bank%d" % c)
+            for t in range(PACK):
+                product(bank[:, t, :], w1, t, xq_words[:, cols(c)], xq_scales[:, cols(c)], True, True)
+            y_banks.append(bank)
+        z_grouped = []
+        for c in range(CHUNKS + 1):
+            if c < CHUNKS:
+                grouped = keep.tile([P, CHUNK, PACK], BF16, name="z_grouped%d" % c, align_bytes=64)
+                nc.vector.tensor_tensor(
+                    out=grouped[:],
+                    in0=y_banks[c][:].rearrange("p t n -> p n t"),
+                    in1=gn_sb[:].unsqueeze(1).to_broadcast([P, CHUNK, PACK]),
+                    op=MULT,
+                )
+                nc.scalar.copy(out=y_sb[:, :, cols(c)], in_=y_banks[c][:])
+                z_grouped.append(grouped)
+            if c > 0:
+                quantize(z_codes[:, cols(c - 1)], z_scales[:, cols(c - 1)], z_grouped[c - 1][:])
+                for t in range(PACK):
+                    product(sweep1[t][:, cols(c - 1)], w2, t, z_codes[:, cols(c - 1)], z_scales[:, cols(c - 1)], True, True)
+
+        residual = []
+        windows = []
+        for t in range(PACK + 1):
+            if t < PACK:
+                u = keep.tile([P, S], F32, name="residual%d" % t)
+                nc.vector.scalar_tensor_tensor(
+                    out=u[:], in0=sweep1[t][:], scalar=-0.5, in1=y_sb[:, t, :], op0=MULT, op1=ADD
+                )
+                residual.append(u)
+            if t > 0:
+                window = keep.tile([P, S], F32, name="window%d" % (t - 1))
+                nc.vector.scalar_tensor_tensor(
+                    out=window[:], in0=residual[t - 1][:], scalar=gn_half[:, t - 1 : t], in1=dinv_sb[:, t - 1, :],
+                    op0=MULT, op1=MULT,
+                )
+                windows.append(window)
+
+        out_rows = out_0.rearrange("(p t) n -> p t n", t=PACK)
+        out_words = out_1[0].rearrange("p n t -> p (n t)").bitcast(I32)
+        out_codes = keep.tile([P, S], U32, name="out_codes", align_bytes=64)
+        out_scales = keep.tile([P, S], U8, name="out_scales", align_bytes=64)
+        z2_grouped = {}
+        banks = {}
+        out_grouped = {}
+
+        def fetch(c):
+            planes = keep.tile([P, PACK, CHUNK], BF16, name="planes%d" % c)
+            lo = c * CHUNK // PER_COLUMN
+            for t in range(PACK):
+                nc.vector.tensor_copy(planes[:, t, :], windows[t][:].indirect(nb_sb[:, lo : lo + CHUNK // PER_COLUMN]))
+            grouped = keep.tile([P, CHUNK, PACK], BF16, name="z2_grouped%d" % c, align_bytes=64)
+            interleave(grouped[:], planes[:])
+            z2_grouped[c] = grouped
+
+        def multiply(c):
+            codes = keep.tile([P, CHUNK], U32, name="z2_codes%d" % c, align_bytes=64)
+            scales = keep.tile([P, CHUNK], U8, name="z2_scales%d" % c, align_bytes=64)
+            quantize(codes[:], scales[:], z2_grouped[c][:])
+            bank = psum.tile([P, PACK, CHUNK], F32, name="sweep2", tag="bank%d" % c)
+            for t in range(PACK):
+                if c > 0:
+                    product(bank[:, t, :], w1, t, xq_words[:, cols(c)], xq_scales[:, cols(c)], True, False)
+                product(bank[:, t, :], w2, t, codes[:], scales[:], c == 0, True)
+            banks[c] = bank
+
+        def finish(c):
+            result = keep.tile([P, PACK, CHUNK], F32, name="result%d" % c)
+            if c == 0:
+                summed = keep.tile([P, PACK, CHUNK], F32, name="summed")
+                nc.vector.tensor_tensor(out=summed[:], in0=banks[c][:], in1=y_sb[:, :, cols(c)], op=ADD)
+                source = summed
+            else:
+                source = banks[c]
+            nc.vector.tensor_tensor(out=result[:], in0=source[:], in1=dinv_sb[:, :, cols(c)], op=MULT)
+            nc.sync.dma_start(out=out_rows[:, :, cols(c)], in_=result[:])
+            grouped = keep.tile([P, CHUNK, PACK], BF16, name="out_grouped%d" % c, align_bytes=64)
+            interleave(grouped[:], result[:])
+            out_grouped[c] = grouped
+
+        def hand_on(c):
+            quantize(out_codes[:, cols(c)], out_scales[:, cols(c)], out_grouped[c][:])
+            nc.sync.dma_start(out=out_words[:, cols(c)], in_=out_codes[:, cols(c)].bitcast(I32))
+
+        stages = [fetch, multiply, finish, hand_on]
+        for step in range(CHUNKS + len(stages) - 1):
+            for depth, stage in enumerate(stages):
+                if 0 <= step - depth < CHUNKS:
+                    stage(step - depth)
+
+        scale_rows = out_2[0].bitcast(I32)
+        for q in range(4):
+            queue = nc.sync if q % 2 == 0 else nc.scalar
+            queue.dma_start(out=scale_rows[4 * q : 4 * q + 4, :], in_=out_scales[32 * q : 32 * q + 4, :].bitcast(I32))

@@ -12,6 +12,7 @@ FP8X4 = mybir.dt.float8_e4m3fn_x4
 FP4X4 = mybir.dt.float4_e2m1fn_x4
 MULT = mybir.AluOpType.mult
 ADD = mybir.AluOpType.add
+COPY = mybir.ActivationFunctionType.Copy
 
 P = 128
 PACK = 4
@@ -36,8 +37,8 @@ def tile_picked_jacobi2_none_po_kernel(
         def cols(c):
             return slice(c * CHUNK, (c + 1) * CHUNK)
 
-        def load_scale_rows(queue, scales, name):
-            raw = keep.tile([P, H], U8, name=name)
+        def load_scale_rows(queue, scales, name, tag):
+            raw = keep.tile([P, H], U8, name=name, tag=tag)
             rows = scales[0].bitcast(I32)
             for q in range(4):
                 queue.dma_start(
@@ -46,14 +47,14 @@ def tile_picked_jacobi2_none_po_kernel(
                 )
             return raw
 
-        def deal(words_raw, scales_raw, name):
-            words = keep.tile([P, 2 * H], U8, name=name + "_words", align_bytes=64)
-            scales = keep.tile([P, H], U8, name=name + "_scales", align_bytes=64)
-            nc.vector.tensor_copy(
+        def deal(engine, words_raw, scales_raw, name, words_tag, scales_tag):
+            words = keep.tile([P, 2 * H], U8, name=name + "_words", tag=words_tag, align_bytes=64)
+            scales = keep.tile([P, H], U8, name=name + "_scales", tag=scales_tag, align_bytes=64)
+            engine.tensor_copy(
                 out=words[:].rearrange("p (t m b) -> p t m b", t=PACK, b=2),
                 in_=words_raw[:].rearrange("p (m t b) -> p t m b", t=PACK, b=2),
             )
-            nc.vector.tensor_copy(
+            engine.tensor_copy(
                 out=scales[:].rearrange("p (t m) -> p t m", t=PACK),
                 in_=scales_raw[:].rearrange("p (m t) -> p t m", t=PACK),
             )
@@ -82,10 +83,10 @@ def tile_picked_jacobi2_none_po_kernel(
 
         offs_sb = lists.tile([P, S // PER_COLUMN], U16, name="offs_sb")
         nb_sb = lists.tile([P, S // PER_COLUMN], U16, name="nb_sb")
-        xs_table = keep.tile([P, T], U8, name="xs_table")
-        xw_table = keep.tile([P, T], U32, name="xw_table")
-        w1_raw = keep.tile([P, 2 * H], U8, name="w1_raw")
-        w2_raw = keep.tile([P, 2 * H], U8, name="w2_raw")
+        xs_table = keep.tile([P, T], U8, name="xs_table", tag="xs_table")
+        xw_table = keep.tile([P, T], U32, name="xw_table", tag="xw_table", align_bytes=64)
+        w1_raw = keep.tile([P, 2 * H], U8, name="w1_raw", tag="w1_raw")
+        w2_raw = keep.tile([P, 2 * H], U8, name="w2_raw", tag="w2_raw", align_bytes=64)
         gn_sb = keep.tile([P, PACK], F32, name="gn_sb")
         xq_scales = keep.tile([P, S], U8, name="xq_scales", align_bytes=64)
 
@@ -94,33 +95,29 @@ def tile_picked_jacobi2_none_po_kernel(
             out=xs_table[:].bitcast(I32),
             in_=x_scales[0].bitcast(I32).unsqueeze(1).to_broadcast([16, 8, T // 4]),
         )
-        nc.scalar.dma_start(out=w1_raw[:].bitcast(I32), in_=w1_words[0].bitcast(I32))
-        w1s_raw = load_scale_rows(nc.scalar, w1_scales, "w1s_raw")
+        nc.sync.dma_start(out=w1_raw[:].bitcast(I32), in_=w1_words[0].bitcast(I32))
+        w1s_raw = load_scale_rows(nc.sync, w1_scales, "w1s_raw", "w1s_raw")
         nc.sync.dma_start(
             out=xw_table[:].bitcast(I32), in_=x_words[0].rearrange("p n t -> p (n t)").bitcast(I32)
         )
         nc.sync.dma_start(out=w2_raw[:].bitcast(I32), in_=w2_words[0].bitcast(I32))
         nc.sync.dma_start(out=gn_sb[:], in_=gn.rearrange("(p t) o -> p (t o)", t=PACK))
         nc.sync.dma_start(nb_sb[:], nb)
-        w2s_raw = keep.tile([P, H], U8, name="w2s_raw")
-        nc.vector.memset(w2s_raw[:].bitcast(I32), 0)
         nc.vector.memset(xq_scales[:].bitcast(I32), 0)
-        for q in range(4):
-            nc.gpsimd.dma_start(
-                out=w2s_raw[32 * q : 32 * q + 4, :].bitcast(I32), in_=w2_scales[0].bitcast(I32)[4 * q : 4 * q + 4, :]
-            )
 
-        xs_picked = keep.tile([P, S], U8, name="xs_picked", tag="late")
+        xs_picked = keep.tile([P, S], U8, name="xs_picked")
         nc.vector.tensor_copy(xs_picked[:], xs_table[:].indirect(offs_sb[:]))
         for q in range(4):
             nc.scalar.dma_start(
                 out=xq_scales[32 * q : 32 * q + 4, :].bitcast(I32),
                 in_=xs_picked[32 * q : 32 * q + 32 : 8, :].bitcast(I32),
             )
-        dinv_sb = keep.tile([P, PACK, S], F32, name="dinv_sb", tag="late")
-        nc.sync.dma_start(out=dinv_sb[:], in_=dinv.rearrange("(p t) n -> p t n", t=PACK))
+        w2s_raw = load_scale_rows(nc.sync, w2_scales, "w2s_raw", "xs_table")
 
-        w1 = deal(w1_raw, w1s_raw, "w1")
+        w1 = deal(nc.vector, w1_raw, w1s_raw, "w1", "w1_words", "w1_scales")
+        dinv_sb = keep.tile([P, PACK, S], F32, name="dinv_sb", tag="w1_raw")
+        for t in range(PACK):
+            nc.sync.dma_start(out=dinv_sb[:, t, :], in_=dinv.rearrange("(p t) n -> p t n", t=PACK)[:, t, :])
         xq_words = keep.tile([P, S], U32, name="xq_words", align_bytes=64)
         half = S // 2
         for h in range(2):
@@ -128,14 +125,14 @@ def tile_picked_jacobi2_none_po_kernel(
                 xq_words[:, h * half : (h + 1) * half],
                 xw_table[:].indirect(offs_sb[:, h * half // PER_COLUMN : (h + 1) * half // PER_COLUMN]),
             )
-        w2 = deal(w2_raw, w2s_raw, "w2")
+        w2 = deal(nc.gpsimd, w2_raw, w2s_raw, "w2", "w2_words", "w2_scales")
         gn_half = keep.tile([P, PACK], F32, name="gn_half")
         nc.vector.tensor_scalar(out=gn_half[:], in0=gn_sb[:], scalar1=-0.5, scalar2=None, op0=MULT)
 
         y_sb = keep.tile([P, PACK, S], F32, name="y_sb")
         z_codes = keep.tile([P, S], U32, name="z_codes", align_bytes=64)
         z_scales = keep.tile([P, S], U8, name="z_scales", align_bytes=64)
-        sweep1 = [psum.tile([P, S], F32, name="sweep1_%d" % t) for t in range(PACK)]
+        sweep1 = [psum.tile([P, S], F32, name="sweep1_%d" % t, tag="row%d" % t) for t in range(PACK)]
         y_banks = []
         for c in range(CHUNKS):
             bank = psum.tile([P, PACK, CHUNK], F32, name="y_bank", tag="bank%d" % c)
@@ -159,22 +156,26 @@ def tile_picked_jacobi2_none_po_kernel(
                 for t in range(PACK):
                     product(sweep1[t][:, cols(c - 1)], w2, t, z_codes[:, cols(c - 1)], z_scales[:, cols(c - 1)], True, True)
 
-        residual = []
         windows = []
-        for t in range(PACK + 1):
-            if t < PACK:
-                u = keep.tile([P, S], F32, name="residual%d" % t)
-                nc.vector.scalar_tensor_tensor(
-                    out=u[:], in0=sweep1[t][:], scalar=-0.5, in1=y_sb[:, t, :], op0=MULT, op1=ADD
+        for t in range(PACK):
+            factor = keep.tile([P, S], F32, name="factor%d" % t)
+            nc.scalar.activation(out=factor[:], in_=dinv_sb[:, t, :], func=COPY, scale=gn_half[:, t : t + 1])
+            residual = keep.tile([P, S], F32, name="residual%d" % t)
+            nc.vector.scalar_tensor_tensor(
+                out=residual[:], in0=sweep1[t][:], scalar=-0.5, in1=y_sb[:, t, :], op0=MULT, op1=ADD
+            )
+            window = keep.tile([P, S], F32, name="window%d" % t)
+            nc.gpsimd.tensor_tensor(out=window[:], in0=residual[:], in1=factor[:], op=MULT)
+            windows.append(window)
+
+        planes = keep.tile([P, PACK, S], BF16, name="planes")
+        for t in range(PACK):
+            width = CHUNK if t == PACK - 1 else half
+            for lo in range(0, S, width):
+                nc.vector.tensor_copy(
+                    planes[:, t, lo : lo + width],
+                    windows[t][:].indirect(nb_sb[:, lo // PER_COLUMN : (lo + width) // PER_COLUMN]),
                 )
-                residual.append(u)
-            if t > 0:
-                window = keep.tile([P, S], F32, name="window%d" % (t - 1))
-                nc.vector.scalar_tensor_tensor(
-                    out=window[:], in0=residual[t - 1][:], scalar=gn_half[:, t - 1 : t], in1=dinv_sb[:, t - 1, :],
-                    op0=MULT, op1=MULT,
-                )
-                windows.append(window)
 
         out_rows = out_0.rearrange("(p t) n -> p t n", t=PACK)
         out_words = out_1[0].rearrange("p n t -> p (n t)").bitcast(I32)
@@ -184,18 +185,24 @@ def tile_picked_jacobi2_none_po_kernel(
         banks = {}
         out_grouped = {}
 
-        def fetch(c):
-            planes = keep.tile([P, PACK, CHUNK], BF16, name="planes%d" % c)
-            lo = c * CHUNK // PER_COLUMN
-            for t in range(PACK):
-                nc.vector.tensor_copy(planes[:, t, :], windows[t][:].indirect(nb_sb[:, lo : lo + CHUNK // PER_COLUMN]))
-            grouped = keep.tile([P, CHUNK, PACK], BF16, name="z2_grouped%d" % c, align_bytes=64)
-            interleave(grouped[:], planes[:])
+        last = CHUNKS - 1
+
+        def regroup(c):
+            grouped = keep.tile([P, CHUNK, PACK], BF16, name="z2_grouped%d" % c, tag="after%d" % c, align_bytes=64)
+            interleave(grouped[:], planes[:, :, cols(c)])
             z2_grouped[c] = grouped
 
         def multiply(c):
             codes = keep.tile([P, CHUNK], U32, name="z2_codes%d" % c, align_bytes=64)
             scales = keep.tile([P, CHUNK], U8, name="z2_scales%d" % c, align_bytes=64)
+            if c == last:
+                banks[c] = [psum.tile([P, CHUNK], F32, name="sweep2_last", tag="row%d" % t) for t in range(PACK)]
+                for t in range(PACK):
+                    product(banks[c][t][:], w1, t, xq_words[:, cols(c)], xq_scales[:, cols(c)], True, False)
+                quantize(codes[:], scales[:], z2_grouped[c][:])
+                for t in range(PACK):
+                    product(banks[c][t][:], w2, t, codes[:], scales[:], False, True)
+                return
             quantize(codes[:], scales[:], z2_grouped[c][:])
             bank = psum.tile([P, PACK, CHUNK], F32, name="sweep2", tag="bank%d" % c)
             for t in range(PACK):
@@ -205,14 +212,16 @@ def tile_picked_jacobi2_none_po_kernel(
             banks[c] = bank
 
         def finish(c):
-            result = keep.tile([P, PACK, CHUNK], F32, name="result%d" % c)
-            if c == 0:
-                summed = keep.tile([P, PACK, CHUNK], F32, name="summed")
+            result = keep.tile([P, PACK, CHUNK], F32, name="result%d" % c, tag="after%d" % (c + 2), align_bytes=64)
+            if c == last:
+                for t in range(PACK):
+                    nc.vector.tensor_tensor(out=result[:, t, :], in0=banks[c][t][:], in1=dinv_sb[:, t, cols(c)], op=MULT)
+            elif c == 0:
+                summed = keep.tile([P, PACK, CHUNK], F32, name="summed", tag="after1", align_bytes=64)
                 nc.vector.tensor_tensor(out=summed[:], in0=banks[c][:], in1=y_sb[:, :, cols(c)], op=ADD)
-                source = summed
+                nc.vector.tensor_tensor(out=result[:], in0=summed[:], in1=dinv_sb[:, :, cols(c)], op=MULT)
             else:
-                source = banks[c]
-            nc.vector.tensor_tensor(out=result[:], in0=source[:], in1=dinv_sb[:, :, cols(c)], op=MULT)
+                nc.vector.tensor_tensor(out=result[:], in0=banks[c][:], in1=dinv_sb[:, :, cols(c)], op=MULT)
             nc.sync.dma_start(out=out_rows[:, :, cols(c)], in_=result[:])
             grouped = keep.tile([P, CHUNK, PACK], BF16, name="out_grouped%d" % c, align_bytes=64)
             interleave(grouped[:], result[:])
@@ -222,11 +231,9 @@ def tile_picked_jacobi2_none_po_kernel(
             quantize(out_codes[:, cols(c)], out_scales[:, cols(c)], out_grouped[c][:])
             nc.sync.dma_start(out=out_words[:, cols(c)], in_=out_codes[:, cols(c)].bitcast(I32))
 
-        stages = [fetch, multiply, finish, hand_on]
-        for step in range(CHUNKS + len(stages) - 1):
-            for depth, stage in enumerate(stages):
-                if 0 <= step - depth < CHUNKS:
-                    stage(step - depth)
+        for stage in (regroup, multiply, finish, hand_on):
+            for c in range(CHUNKS):
+                stage(c)
 
         scale_rows = out_2[0].bitcast(I32)
         for q in range(4):

@@ -37,28 +37,23 @@ def tile_picked_jacobi2_none_po_kernel(
         def cols(c):
             return slice(c * CHUNK, (c + 1) * CHUNK)
 
-        def load_scale_rows(queue, scales, name, tag):
-            raw = keep.tile([P, H], U8, name=name, tag=tag)
+        def load_scale_rows(queues, scales, name, tag):
+            raw = keep.tile([P, H], U8, name=name, tag=tag, align_bytes=64)
             rows = scales[0].bitcast(I32)
             for q in range(4):
-                queue.dma_start(
+                queues[q].dma_start(
                     out=raw[32 * q : 32 * q + 32, :].bitcast(I32),
                     in_=rows[4 * q : 4 * q + 4, :].unsqueeze(0).to_broadcast([8, 4, H // 4]),
                 )
             return raw
 
-        def deal(engine, words_raw, scales_raw, name, words_tag, scales_tag):
-            words = keep.tile([P, 2 * H], U8, name=name + "_words", tag=words_tag, align_bytes=64)
-            scales = keep.tile([P, H], U8, name=name + "_scales", tag=scales_tag, align_bytes=64)
-            engine.tensor_copy(
-                out=words[:].rearrange("p (t m b) -> p t m b", t=PACK, b=2),
-                in_=words_raw[:].rearrange("p (m t b) -> p t m b", t=PACK, b=2),
+        def deal(raw, width, name, tag):
+            dealt = keep.tile([P, width * H], U8, name=name, tag=tag, align_bytes=64)
+            nc.vector.tensor_copy(
+                out=dealt[:].rearrange("p (t m b) -> p t m b", t=PACK, b=width),
+                in_=raw[:].rearrange("p (m t b) -> p t m b", t=PACK, b=width),
             )
-            engine.tensor_copy(
-                out=scales[:].rearrange("p (t m) -> p t m", t=PACK),
-                in_=scales_raw[:].rearrange("p (m t) -> p t m", t=PACK),
-            )
-            return words, scales
+            return dealt
 
         def product(bank, weights, t, codes, scales, start, stop):
             words, wscales = weights
@@ -83,39 +78,40 @@ def tile_picked_jacobi2_none_po_kernel(
 
         offs_sb = lists.tile([P, S // PER_COLUMN], U16, name="offs_sb")
         nb_sb = lists.tile([P, S // PER_COLUMN], U16, name="nb_sb")
-        xs_table = keep.tile([P, T], U8, name="xs_table", tag="xs_table")
+        xs_table = keep.tile([P, T], U8, name="xs_table", tag="xs_table", align_bytes=64)
         xw_table = keep.tile([P, T], U32, name="xw_table", tag="xw_table", align_bytes=64)
-        w1_raw = keep.tile([P, 2 * H], U8, name="w1_raw", tag="w1_raw")
+        w1_raw = keep.tile([P, 2 * H], U8, name="w1_raw", tag="w1_raw", align_bytes=64)
         w2_raw = keep.tile([P, 2 * H], U8, name="w2_raw", tag="w2_raw", align_bytes=64)
         gn_sb = keep.tile([P, PACK], F32, name="gn_sb")
         xq_scales = keep.tile([P, S], U8, name="xq_scales", align_bytes=64)
 
         nc.sync.dma_start(offs_sb[:], offs)
-        nc.sync.dma_start(
+        nc.scalar.dma_start(
             out=xs_table[:].bitcast(I32),
             in_=x_scales[0].bitcast(I32).unsqueeze(1).to_broadcast([16, 8, T // 4]),
         )
         nc.sync.dma_start(out=w1_raw[:].bitcast(I32), in_=w1_words[0].bitcast(I32))
-        w1s_raw = load_scale_rows(nc.sync, w1_scales, "w1s_raw", "w1s_raw")
+        w1s_raw = load_scale_rows([nc.sync, nc.scalar, nc.scalar, nc.scalar], w1_scales, "w1s_raw", "w1s_raw")
         nc.sync.dma_start(
             out=xw_table[:].bitcast(I32), in_=x_words[0].rearrange("p n t -> p (n t)").bitcast(I32)
         )
         nc.sync.dma_start(out=w2_raw[:].bitcast(I32), in_=w2_words[0].bitcast(I32))
-        nc.sync.dma_start(out=gn_sb[:], in_=gn.rearrange("(p t) o -> p (t o)", t=PACK))
         nc.sync.dma_start(nb_sb[:], nb)
-        nc.vector.memset(xq_scales[:].bitcast(I32), 0)
+        nc.gpsimd.dma_start(out=gn_sb[:], in_=gn.rearrange("(p t) o -> p (t o)", t=PACK))
+        nc.gpsimd.memset(xq_scales[:].bitcast(I32), 0)
 
-        xs_picked = keep.tile([P, S], U8, name="xs_picked")
+        xs_picked = keep.tile([P, S], U8, name="xs_picked", tag="xs_picked")
         nc.vector.tensor_copy(xs_picked[:], xs_table[:].indirect(offs_sb[:]))
         for q in range(4):
-            nc.scalar.dma_start(
+            queue = nc.scalar if q % 2 == 0 else nc.sync
+            queue.dma_start(
                 out=xq_scales[32 * q : 32 * q + 4, :].bitcast(I32),
                 in_=xs_picked[32 * q : 32 * q + 32 : 8, :].bitcast(I32),
             )
-        w2s_raw = load_scale_rows(nc.sync, w2_scales, "w2s_raw", "xs_table")
 
-        w1 = deal(nc.vector, w1_raw, w1s_raw, "w1", "w1_words", "w1_scales")
-        dinv_sb = keep.tile([P, PACK, S], F32, name="dinv_sb", tag="w1_raw")
+        w2s_raw = load_scale_rows([nc.sync] * 4, w2_scales, "w2s_raw", "xs_table")
+        w1 = (deal(w1_raw, 2, "w1_words", "w1_words"), deal(w1s_raw, 1, "w1_scales", "w1_scales"))
+        dinv_sb = keep.tile([P, PACK, S], F32, name="dinv_sb", tag="w1_raw", align_bytes=64)
         for t in range(PACK):
             nc.sync.dma_start(out=dinv_sb[:, t, :], in_=dinv.rearrange("(p t) n -> p t n", t=PACK)[:, t, :])
         xq_words = keep.tile([P, S], U32, name="xq_words", align_bytes=64)
@@ -125,9 +121,9 @@ def tile_picked_jacobi2_none_po_kernel(
                 xq_words[:, h * half : (h + 1) * half],
                 xw_table[:].indirect(offs_sb[:, h * half // PER_COLUMN : (h + 1) * half // PER_COLUMN]),
             )
-        w2 = deal(nc.gpsimd, w2_raw, w2s_raw, "w2", "w2_words", "w2_scales")
+        w2_dealt = deal(w2_raw, 2, "w2_words", "xw_table")
         gn_half = keep.tile([P, PACK], F32, name="gn_half")
-        nc.vector.tensor_scalar(out=gn_half[:], in0=gn_sb[:], scalar1=-0.5, scalar2=None, op0=MULT)
+        nc.gpsimd.tensor_scalar(out=gn_half[:], in0=gn_sb[:], scalar1=-0.5, scalar2=None, op0=MULT)
 
         y_sb = keep.tile([P, PACK, S], F32, name="y_sb")
         z_codes = keep.tile([P, S], U32, name="z_codes", align_bytes=64)
@@ -140,21 +136,25 @@ def tile_picked_jacobi2_none_po_kernel(
                 product(bank[:, t, :], w1, t, xq_words[:, cols(c)], xq_scales[:, cols(c)], True, True)
             y_banks.append(bank)
         z_grouped = []
-        for c in range(CHUNKS + 1):
-            if c < CHUNKS:
-                grouped = keep.tile([P, CHUNK, PACK], BF16, name="z_grouped%d" % c, align_bytes=64)
+        for h in range(2):
+            grouped = keep.tile([P, half, PACK], BF16, name="z_grouped", tag="z_grouped%d" % h, align_bytes=64)
+            for i in range(2):
+                c = 2 * h + i
                 nc.vector.tensor_tensor(
-                    out=grouped[:],
+                    out=grouped[:, cols(i), :],
                     in0=y_banks[c][:].rearrange("p t n -> p n t"),
                     in1=gn_sb[:].unsqueeze(1).to_broadcast([P, CHUNK, PACK]),
                     op=MULT,
                 )
                 nc.scalar.copy(out=y_sb[:, :, cols(c)], in_=y_banks[c][:])
-                z_grouped.append(grouped)
-            if c > 0:
-                quantize(z_codes[:, cols(c - 1)], z_scales[:, cols(c - 1)], z_grouped[c - 1][:])
-                for t in range(PACK):
-                    product(sweep1[t][:, cols(c - 1)], w2, t, z_codes[:, cols(c - 1)], z_scales[:, cols(c - 1)], True, True)
+            z_grouped.append(grouped)
+        halves = [slice(0, half), slice(half, S)]
+        quantize(z_codes[:, halves[0]], z_scales[:, halves[0]], z_grouped[0][:])
+        w2 = (w2_dealt, deal(w2s_raw, 1, "w2_scales", "z_grouped0"))
+        quantize(z_codes[:, halves[1]], z_scales[:, halves[1]], z_grouped[1][:])
+        for h in halves:
+            for t in range(PACK):
+                product(sweep1[t][:, h], w2, t, z_codes[:, h], z_scales[:, h], True, True)
 
         windows = []
         for t in range(PACK):
@@ -168,72 +168,63 @@ def tile_picked_jacobi2_none_po_kernel(
             nc.gpsimd.tensor_tensor(out=window[:], in0=residual[:], in1=factor[:], op=MULT)
             windows.append(window)
 
-        planes = keep.tile([P, PACK, S], BF16, name="planes")
-        for t in range(PACK):
-            width = CHUNK if t == PACK - 1 else half
-            for lo in range(0, S, width):
-                nc.vector.tensor_copy(
-                    planes[:, t, lo : lo + width],
-                    windows[t][:].indirect(nb_sb[:, lo // PER_COLUMN : (lo + width) // PER_COLUMN]),
-                )
+        def fetch(dst, t, lo, width):
+            nc.vector.tensor_copy(dst, windows[t][:].indirect(nb_sb[:, lo // PER_COLUMN : (lo + width) // PER_COLUMN]))
+
+        low_planes = keep.tile([P, 2, S], BF16, name="low_planes")
+        for t in range(2):
+            for lo in range(0, S, half):
+                fetch(low_planes[:, t, lo : lo + half], t, lo, half)
+        z2_grouped = []
+        for c in range(CHUNKS):
+            grouped = keep.tile([P, CHUNK, PACK], BF16, name="z2_grouped%d" % c, tag="after%d" % c, align_bytes=64)
+            nc.scalar.copy(out=grouped[:, :, 0:2], in_=low_planes[:, :, cols(c)].rearrange("p t n -> p n t"))
+            z2_grouped.append(grouped)
+        high_planes = keep.tile([P, 2, S], BF16, name="high_planes")
+        for lo in range(0, S, half):
+            fetch(high_planes[:, 0, lo : lo + half], 2, lo, half)
+        for c in range(CHUNKS):
+            fetch(high_planes[:, 1, cols(c)], 3, c * CHUNK, CHUNK)
+            nc.scalar.copy(out=z2_grouped[c][:, :, 2:4], in_=high_planes[:, :, cols(c)].rearrange("p t n -> p n t"))
 
         out_rows = out_0.rearrange("(p t) n -> p t n", t=PACK)
         out_words = out_1[0].rearrange("p n t -> p (n t)").bitcast(I32)
         out_codes = keep.tile([P, S], U32, name="out_codes", align_bytes=64)
         out_scales = keep.tile([P, S], U8, name="out_scales", align_bytes=64)
-        z2_grouped = {}
-        banks = {}
-        out_grouped = {}
-
-        last = CHUNKS - 1
-
-        def regroup(c):
-            grouped = keep.tile([P, CHUNK, PACK], BF16, name="z2_grouped%d" % c, tag="after%d" % c, align_bytes=64)
-            interleave(grouped[:], planes[:, :, cols(c)])
-            z2_grouped[c] = grouped
-
-        def multiply(c):
+        bank_tags = [["bank0"], ["bank1"], ["bank2", "bank3"], ["row0", "row1"]]
+        banks = []
+        for c in range(CHUNKS):
             codes = keep.tile([P, CHUNK], U32, name="z2_codes%d" % c, align_bytes=64)
             scales = keep.tile([P, CHUNK], U8, name="z2_scales%d" % c, align_bytes=64)
-            if c == last:
-                banks[c] = [psum.tile([P, CHUNK], F32, name="sweep2_last", tag="row%d" % t) for t in range(PACK)]
-                for t in range(PACK):
-                    product(banks[c][t][:], w1, t, xq_words[:, cols(c)], xq_scales[:, cols(c)], True, False)
-                quantize(codes[:], scales[:], z2_grouped[c][:])
-                for t in range(PACK):
-                    product(banks[c][t][:], w2, t, codes[:], scales[:], False, True)
-                return
             quantize(codes[:], scales[:], z2_grouped[c][:])
-            bank = psum.tile([P, PACK, CHUNK], F32, name="sweep2", tag="bank%d" % c)
+            per_bank = PACK // len(bank_tags[c])
+            tiles = [psum.tile([P, per_bank, CHUNK], F32, name="sweep2", tag=tag) for tag in bank_tags[c]]
             for t in range(PACK):
+                target = tiles[t // per_bank][:, t % per_bank, :]
                 if c > 0:
-                    product(bank[:, t, :], w1, t, xq_words[:, cols(c)], xq_scales[:, cols(c)], True, False)
-                product(bank[:, t, :], w2, t, codes[:], scales[:], c == 0, True)
-            banks[c] = bank
+                    product(target, w1, t, xq_words[:, cols(c)], xq_scales[:, cols(c)], True, False)
+                product(target, w2, t, codes[:], scales[:], c == 0, True)
+            banks.append(tiles)
 
-        def finish(c):
-            result = keep.tile([P, PACK, CHUNK], F32, name="result%d" % c, tag="after%d" % (c + 2), align_bytes=64)
-            if c == last:
-                for t in range(PACK):
-                    nc.vector.tensor_tensor(out=result[:, t, :], in0=banks[c][t][:], in1=dinv_sb[:, t, cols(c)], op=MULT)
-            elif c == 0:
-                summed = keep.tile([P, PACK, CHUNK], F32, name="summed", tag="after1", align_bytes=64)
-                nc.vector.tensor_tensor(out=summed[:], in0=banks[c][:], in1=y_sb[:, :, cols(c)], op=ADD)
-                nc.vector.tensor_tensor(out=result[:], in0=summed[:], in1=dinv_sb[:, :, cols(c)], op=MULT)
-            else:
-                nc.vector.tensor_tensor(out=result[:], in0=banks[c][:], in1=dinv_sb[:, :, cols(c)], op=MULT)
+        summed = keep.tile([P, PACK, CHUNK], F32, name="summed", tag="after2", align_bytes=64)
+        nc.vector.tensor_tensor(out=summed[:], in0=banks[0][0][:], in1=y_sb[:, :, cols(0)], op=ADD)
+        sources = [[summed]] + banks[1:]
+        order = [1, 0, 2, 3]
+        out_grouped = keep.tile([P, S, PACK], BF16, name="out_grouped", align_bytes=64)
+        for c in order:
+            result = keep.tile(
+                [P, PACK, CHUNK], F32, name="result%d" % c, tag="after%d" % (c + 2 if c else 6), align_bytes=64
+            )
+            per_bank = PACK // len(sources[c])
+            for b, source in enumerate(sources[c]):
+                rows = slice(b * per_bank, (b + 1) * per_bank)
+                nc.vector.tensor_tensor(out=result[:, rows, :], in0=source[:], in1=dinv_sb[:, rows, cols(c)], op=MULT)
             nc.sync.dma_start(out=out_rows[:, :, cols(c)], in_=result[:])
-            grouped = keep.tile([P, CHUNK, PACK], BF16, name="out_grouped%d" % c, align_bytes=64)
-            interleave(grouped[:], result[:])
-            out_grouped[c] = grouped
-
-        def hand_on(c):
-            quantize(out_codes[:, cols(c)], out_scales[:, cols(c)], out_grouped[c][:])
-            nc.sync.dma_start(out=out_words[:, cols(c)], in_=out_codes[:, cols(c)].bitcast(I32))
-
-        for stage in (regroup, multiply, finish, hand_on):
-            for c in range(CHUNKS):
-                stage(c)
+            interleave(out_grouped[:, cols(c), :], result[:])
+        for piece in (halves[0], cols(2), cols(3)):
+            quantize(out_codes[:, piece], out_scales[:, piece], out_grouped[:, piece, :])
+        for h in halves:
+            nc.sync.dma_start(out=out_words[:, h], in_=out_codes[:, h].bitcast(I32))
 
         scale_rows = out_2[0].bitcast(I32)
         for q in range(4):

@@ -47,9 +47,9 @@ def tile_picked_jacobi2_none_po_kernel(
                 )
             return raw
 
-        def deal(raw, width, name, tag):
-            dealt = keep.tile([P, width * H], U8, name=name, tag=tag, align_bytes=64)
-            nc.vector.tensor_copy(
+        def deal(engine, raw, width, name):
+            dealt = keep.tile([P, width * H], U8, name=name, align_bytes=64)
+            engine.tensor_copy(
                 out=dealt[:].rearrange("p (t m b) -> p t m b", t=PACK, b=width),
                 in_=raw[:].rearrange("p (m t b) -> p t m b", t=PACK, b=width),
             )
@@ -86,31 +86,30 @@ def tile_picked_jacobi2_none_po_kernel(
         xq_scales = keep.tile([P, S], U8, name="xq_scales", align_bytes=64)
 
         nc.sync.dma_start(offs_sb[:], offs)
-        nc.scalar.dma_start(
+        nc.sync.dma_start(
             out=xs_table[:].bitcast(I32),
             in_=x_scales[0].bitcast(I32).unsqueeze(1).to_broadcast([16, 8, T // 4]),
         )
         nc.sync.dma_start(out=w1_raw[:].bitcast(I32), in_=w1_words[0].bitcast(I32))
-        w1s_raw = load_scale_rows([nc.sync, nc.scalar, nc.scalar, nc.scalar], w1_scales, "w1s_raw", "w1s_raw")
+        w1s_raw = load_scale_rows([nc.sync] * 4, w1_scales, "w1s_raw", "w1s_raw")
         nc.sync.dma_start(
             out=xw_table[:].bitcast(I32), in_=x_words[0].rearrange("p n t -> p (n t)").bitcast(I32)
         )
         nc.sync.dma_start(out=w2_raw[:].bitcast(I32), in_=w2_words[0].bitcast(I32))
         nc.sync.dma_start(nb_sb[:], nb)
         nc.gpsimd.dma_start(out=gn_sb[:], in_=gn.rearrange("(p t) o -> p (t o)", t=PACK))
-        nc.gpsimd.memset(xq_scales[:].bitcast(I32), 0)
+        nc.vector.memset(xq_scales[:].bitcast(I32), 0)
 
         xs_picked = keep.tile([P, S], U8, name="xs_picked", tag="xs_picked")
         nc.vector.tensor_copy(xs_picked[:], xs_table[:].indirect(offs_sb[:]))
         for q in range(4):
-            queue = nc.scalar if q % 2 == 0 else nc.sync
-            queue.dma_start(
+            nc.scalar.dma_start(
                 out=xq_scales[32 * q : 32 * q + 4, :].bitcast(I32),
                 in_=xs_picked[32 * q : 32 * q + 32 : 8, :].bitcast(I32),
             )
 
         w2s_raw = load_scale_rows([nc.sync] * 4, w2_scales, "w2s_raw", "xs_table")
-        w1 = (deal(w1_raw, 2, "w1_words", "w1_words"), deal(w1s_raw, 1, "w1_scales", "w1_scales"))
+        w1 = (deal(nc.vector, w1_raw, 2, "w1_words"), deal(nc.vector, w1s_raw, 1, "w1_scales"))
         dinv_sb = keep.tile([P, PACK, S], F32, name="dinv_sb", tag="w1_raw", align_bytes=64)
         for t in range(PACK):
             nc.sync.dma_start(out=dinv_sb[:, t, :], in_=dinv.rearrange("(p t) n -> p t n", t=PACK)[:, t, :])
@@ -121,7 +120,7 @@ def tile_picked_jacobi2_none_po_kernel(
                 xq_words[:, h * half : (h + 1) * half],
                 xw_table[:].indirect(offs_sb[:, h * half // PER_COLUMN : (h + 1) * half // PER_COLUMN]),
             )
-        w2_dealt = deal(w2_raw, 2, "w2_words", "xw_table")
+        w2 = (deal(nc.gpsimd, w2_raw, 2, "w2_words"), deal(nc.gpsimd, w2s_raw, 1, "w2_scales"))
         gn_half = keep.tile([P, PACK], F32, name="gn_half")
         nc.gpsimd.tensor_scalar(out=gn_half[:], in0=gn_sb[:], scalar1=-0.5, scalar2=None, op0=MULT)
 
@@ -135,38 +134,51 @@ def tile_picked_jacobi2_none_po_kernel(
             for t in range(PACK):
                 product(bank[:, t, :], w1, t, xq_words[:, cols(c)], xq_scales[:, cols(c)], True, True)
             y_banks.append(bank)
-        z_grouped = []
-        for h in range(2):
-            grouped = keep.tile([P, half, PACK], BF16, name="z_grouped", tag="z_grouped%d" % h, align_bytes=64)
-            for i in range(2):
-                c = 2 * h + i
-                nc.vector.tensor_tensor(
-                    out=grouped[:, cols(i), :],
-                    in0=y_banks[c][:].rearrange("p t n -> p n t"),
-                    in1=gn_sb[:].unsqueeze(1).to_broadcast([P, CHUNK, PACK]),
-                    op=MULT,
-                )
-                nc.scalar.copy(out=y_sb[:, :, cols(c)], in_=y_banks[c][:])
-            z_grouped.append(grouped)
-        halves = [slice(0, half), slice(half, S)]
-        quantize(z_codes[:, halves[0]], z_scales[:, halves[0]], z_grouped[0][:])
-        w2 = (w2_dealt, deal(w2s_raw, 1, "w2_scales", "z_grouped0"))
-        quantize(z_codes[:, halves[1]], z_scales[:, halves[1]], z_grouped[1][:])
-        for h in halves:
-            for t in range(PACK):
-                product(sweep1[t][:, h], w2, t, z_codes[:, h], z_scales[:, h], True, True)
-
-        windows = []
-        for t in range(PACK):
-            factor = keep.tile([P, S], F32, name="factor%d" % t)
-            nc.scalar.activation(out=factor[:], in_=dinv_sb[:, t, :], func=COPY, scale=gn_half[:, t : t + 1])
-            residual = keep.tile([P, S], F32, name="residual%d" % t)
-            nc.vector.scalar_tensor_tensor(
-                out=residual[:], in0=sweep1[t][:], scalar=-0.5, in1=y_sb[:, t, :], op0=MULT, op1=ADD
+        z_grouped = keep.tile([P, S, PACK], BF16, name="z_grouped", align_bytes=64)
+        for c in range(CHUNKS):
+            nc.vector.tensor_tensor(
+                out=z_grouped[:, cols(c), :],
+                in0=y_banks[c][:].rearrange("p t n -> p n t"),
+                in1=gn_sb[:].unsqueeze(1).to_broadcast([P, CHUNK, PACK]),
+                op=MULT,
             )
-            window = keep.tile([P, S], F32, name="window%d" % t)
-            nc.gpsimd.tensor_tensor(out=window[:], in0=residual[:], in1=factor[:], op=MULT)
-            windows.append(window)
+            nc.scalar.copy(out=y_sb[:, :, cols(c)], in_=y_banks[c][:])
+        factors = [keep.tile([P, S], F32, name="factor%d" % t) for t in range(PACK)]
+        residuals = [keep.tile([P, S], F32, name="residual%d" % t) for t in range(PACK)]
+        windows = [keep.tile([P, S], F32, name="window%d" % t) for t in range(PACK)]
+        for t in range(PACK):
+            nc.scalar.activation(out=factors[t][:], in_=dinv_sb[:, t, :], func=COPY, scale=gn_half[:, t : t + 1])
+
+        def update(t, piece):
+            nc.vector.scalar_tensor_tensor(
+                out=residuals[t][:, piece], in0=sweep1[t][:, piece], scalar=-0.5, in1=y_sb[:, t, piece],
+                op0=MULT, op1=ADD,
+            )
+            nc.gpsimd.tensor_tensor(
+                out=windows[t][:, piece], in0=residuals[t][:, piece], in1=factors[t][:, piece], op=MULT
+            )
+
+        def quantize_z(piece):
+            quantize(z_codes[:, piece], z_scales[:, piece], z_grouped[:, piece, :])
+
+        def multiply_z(piece):
+            for t in range(PACK):
+                product(sweep1[t][:, piece], w2, t, z_codes[:, piece], z_scales[:, piece], True, True)
+
+        low, high = slice(0, half), slice(half, S)
+        pieces = [low, cols(2), cols(3)]
+        quantize_z(low)
+        multiply_z(low)
+        update(0, low)
+        quantize_z(cols(2))
+        multiply_z(cols(2))
+        quantize_z(cols(3))
+        update(1, low)
+        multiply_z(cols(3))
+        update(0, high)
+        update(1, high)
+        update(2, slice(0, S))
+        update(3, slice(0, S))
 
         def fetch(dst, t, lo, width):
             nc.vector.tensor_copy(dst, windows[t][:].indirect(nb_sb[:, lo // PER_COLUMN : (lo + width) // PER_COLUMN]))
@@ -180,7 +192,7 @@ def tile_picked_jacobi2_none_po_kernel(
             grouped = keep.tile([P, CHUNK, PACK], BF16, name="z2_grouped%d" % c, tag="after%d" % c, align_bytes=64)
             nc.scalar.copy(out=grouped[:, :, 0:2], in_=low_planes[:, :, cols(c)].rearrange("p t n -> p n t"))
             z2_grouped.append(grouped)
-        high_planes = keep.tile([P, 2, S], BF16, name="high_planes")
+        high_planes = keep.tile([P, 2, S], BF16, name="high_planes", tag="high_planes", align_bytes=64)
         for lo in range(0, S, half):
             fetch(high_planes[:, 0, lo : lo + half], 2, lo, half)
         for c in range(CHUNKS):
@@ -191,7 +203,7 @@ def tile_picked_jacobi2_none_po_kernel(
         out_words = out_1[0].rearrange("p n t -> p (n t)").bitcast(I32)
         out_codes = keep.tile([P, S], U32, name="out_codes", align_bytes=64)
         out_scales = keep.tile([P, S], U8, name="out_scales", align_bytes=64)
-        bank_tags = [["bank0"], ["bank1"], ["bank2", "bank3"], ["row0", "row1"]]
+        bank_tags = [["bank0"], ["bank1"], ["bank2", "bank3"], ["row0", "row1", "row2", "row3"]]
         banks = []
         for c in range(CHUNKS):
             codes = keep.tile([P, CHUNK], U32, name="z2_codes%d" % c, align_bytes=64)
@@ -209,24 +221,29 @@ def tile_picked_jacobi2_none_po_kernel(
         summed = keep.tile([P, PACK, CHUNK], F32, name="summed", tag="after2", align_bytes=64)
         nc.vector.tensor_tensor(out=summed[:], in0=banks[0][0][:], in1=y_sb[:, :, cols(0)], op=ADD)
         sources = [[summed]] + banks[1:]
-        order = [1, 0, 2, 3]
+        order = [0, 1, 2, 3]
+        result_tags = ["after3", "high_planes", "result2", "result3"]
         out_grouped = keep.tile([P, S, PACK], BF16, name="out_grouped", align_bytes=64)
         for c in order:
             result = keep.tile(
-                [P, PACK, CHUNK], F32, name="result%d" % c, tag="after%d" % (c + 2 if c else 6), align_bytes=64
+                [P, PACK, CHUNK], F32, name="result%d" % c, tag=result_tags[c], align_bytes=64
             )
             per_bank = PACK // len(sources[c])
             for b, source in enumerate(sources[c]):
                 rows = slice(b * per_bank, (b + 1) * per_bank)
-                nc.vector.tensor_tensor(out=result[:, rows, :], in0=source[:], in1=dinv_sb[:, rows, cols(c)], op=MULT)
+                engine = nc.gpsimd if c == 0 else nc.vector
+                engine.tensor_tensor(out=result[:, rows, :], in0=source[:], in1=dinv_sb[:, rows, cols(c)], op=MULT)
             nc.sync.dma_start(out=out_rows[:, :, cols(c)], in_=result[:])
-            interleave(out_grouped[:, cols(c), :], result[:])
-        for piece in (halves[0], cols(2), cols(3)):
+            if c == 0:
+                nc.gpsimd.tensor_copy(out=out_grouped[:, cols(c), :], in_=result[:].rearrange("p t n -> p n t"))
+            else:
+                interleave(out_grouped[:, cols(c), :], result[:])
+        for piece in pieces:
             quantize(out_codes[:, piece], out_scales[:, piece], out_grouped[:, piece, :])
-        for h in halves:
+        for h in (slice(0, half), slice(half, S)):
             nc.sync.dma_start(out=out_words[:, h], in_=out_codes[:, h].bitcast(I32))
 
         scale_rows = out_2[0].bitcast(I32)
         for q in range(4):
-            queue = nc.sync if q % 2 == 0 else nc.scalar
+            queue = nc.sync if q == 0 else nc.scalar
             queue.dma_start(out=scale_rows[4 * q : 4 * q + 4, :], in_=out_scales[32 * q : 32 * q + 4, :].bitcast(I32))

@@ -15,14 +15,33 @@ ADD = mybir.AluOpType.add
 COPY = mybir.ActivationFunctionType.Copy
 
 P = 128
-PACK = 4
+PLANES = 4
+QUADRANTS = 4
+QUADRANT = P // QUADRANTS
+BLOCK_PARTITIONS = 8
+BLOCKS = QUADRANT // BLOCK_PARTITIONS
 T = 2048
 S = 512
 H = 512
 CHUNK = 128
 CHUNKS = S // CHUNK
-PER_COLUMN = 16
-FLOPS = 3 * 2 * 512 * 512 * 512
+HALF = S // 2
+OFFSETS_PER_COLUMN = 16
+WORD_BYTES = 4
+FP4_WORD_BYTES = 2
+LINE = 4
+FLOPS = 3 * 2 * H * H * S
+
+
+def chunk(c):
+    return slice(c * CHUNK, (c + 1) * CHUNK)
+
+
+def entries(columns):
+    return slice(columns.start // OFFSETS_PER_COLUMN, columns.stop // OFFSETS_PER_COLUMN)
+
+
+LOW, HIGH, ALL = slice(0, HALF), slice(HALF, S), slice(0, S)
 
 
 def tile_picked_jacobi2_none_po_kernel(
@@ -34,216 +53,233 @@ def tile_picked_jacobi2_none_po_kernel(
         keep = ctx.enter_context(tc.tile_pool(name="keep", bufs=1))
         psum = ctx.enter_context(tc.psum_pool(name="psum", bufs=1))
 
-        def cols(c):
-            return slice(c * CHUNK, (c + 1) * CHUNK)
-
-        def load_scale_rows(queues, scales, name, tag):
+        def load_weight_scales(scales, name, tag):
             raw = keep.tile([P, H], U8, name=name, tag=tag, align_bytes=64)
             rows = scales[0].bitcast(I32)
-            for q in range(4):
-                queues[q].dma_start(
-                    out=raw[32 * q : 32 * q + 32, :].bitcast(I32),
-                    in_=rows[4 * q : 4 * q + 4, :].unsqueeze(0).to_broadcast([8, 4, H // 4]),
+            for q in range(QUADRANTS):
+                nc.sync.dma_start(
+                    out=raw[QUADRANT * q : QUADRANT * (q + 1), :].bitcast(I32),
+                    in_=rows[BLOCKS * q : BLOCKS * (q + 1), :]
+                    .unsqueeze(0)
+                    .to_broadcast([QUADRANT // BLOCKS, BLOCKS, H // WORD_BYTES]),
                 )
             return raw
 
         def deal(engine, raw, width, name):
             dealt = keep.tile([P, width * H], U8, name=name, align_bytes=64)
             engine.tensor_copy(
-                out=dealt[:].rearrange("p (t m b) -> p t m b", t=PACK, b=width),
-                in_=raw[:].rearrange("p (m t b) -> p t m b", t=PACK, b=width),
+                out=dealt[:].rearrange("p (t m b) -> p t m b", t=PLANES, b=width),
+                in_=raw[:].rearrange("p (m t b) -> p t m b", t=PLANES, b=width),
             )
             return dealt
 
-        def product(bank, weights, t, codes, scales, start, stop):
-            words, wscales = weights
+        def product(target, weights, t, codes, scales, start, stop):
+            weight_words, weight_scales = weights
             nc.tensor.matmul_mx(
-                out=bank,
-                lhsT=words[:, 2 * P * t : 2 * P * (t + 1)].bitcast(FP4X4),
-                lhsT_scale=wscales[:, P * t : P * (t + 1)],
+                out=target,
+                lhsT=weight_words[:, FP4_WORD_BYTES * P * t : FP4_WORD_BYTES * P * (t + 1)].bitcast(FP4X4),
+                lhsT_scale=weight_scales[:, P * t : P * (t + 1)],
                 rhs=codes.bitcast(FP8X4),
                 rhs_scale=scales,
                 start=start,
                 stop=stop,
             )
 
-        def interleave(dst, src):
-            nc.scalar.copy(
-                out=dst.rearrange("p (c i) t -> p c t i", i=4),
-                in_=src.rearrange("p t (c i) -> p c t i", i=4),
-            )
-
         def quantize(codes, scales, grouped):
             nc.vector.quantize_mx(out=codes.bitcast(FP8X4), scales=scales, in_=grouped.rearrange("p n t -> p (n t)"))
 
-        offs_sb = lists.tile([P, S // PER_COLUMN], U16, name="offs_sb")
-        nb_sb = lists.tile([P, S // PER_COLUMN], U16, name="nb_sb")
+        offs_sb = lists.tile([P, S // OFFSETS_PER_COLUMN], U16, name="offs_sb")
+        nb_sb = lists.tile([P, S // OFFSETS_PER_COLUMN], U16, name="nb_sb")
         xs_table = keep.tile([P, T], U8, name="xs_table", tag="xs_table", align_bytes=64)
-        xw_table = keep.tile([P, T], U32, name="xw_table", tag="xw_table", align_bytes=64)
-        w1_raw = keep.tile([P, 2 * H], U8, name="w1_raw", tag="w1_raw", align_bytes=64)
-        w2_raw = keep.tile([P, 2 * H], U8, name="w2_raw", tag="w2_raw", align_bytes=64)
-        gn_sb = keep.tile([P, PACK], F32, name="gn_sb")
+        xw_table = keep.tile([P, T], U32, name="xw_table", align_bytes=64)
+        w1_raw = keep.tile([P, FP4_WORD_BYTES * H], U8, name="w1_raw", tag="w1_raw", align_bytes=64)
+        w2_raw = keep.tile([P, FP4_WORD_BYTES * H], U8, name="w2_raw", align_bytes=64)
+        gn_sb = keep.tile([P, PLANES], F32, name="gn_sb")
         xq_scales = keep.tile([P, S], U8, name="xq_scales", align_bytes=64)
 
         nc.sync.dma_start(offs_sb[:], offs)
         nc.sync.dma_start(
             out=xs_table[:].bitcast(I32),
-            in_=x_scales[0].bitcast(I32).unsqueeze(1).to_broadcast([16, 8, T // 4]),
+            in_=x_scales[0]
+            .bitcast(I32)
+            .unsqueeze(1)
+            .to_broadcast([P // BLOCK_PARTITIONS, BLOCK_PARTITIONS, T // WORD_BYTES]),
         )
         nc.sync.dma_start(out=w1_raw[:].bitcast(I32), in_=w1_words[0].bitcast(I32))
-        w1s_raw = load_scale_rows([nc.sync] * 4, w1_scales, "w1s_raw", "w1s_raw")
-        nc.sync.dma_start(
-            out=xw_table[:].bitcast(I32), in_=x_words[0].rearrange("p n t -> p (n t)").bitcast(I32)
-        )
+        w1s_raw = load_weight_scales(w1_scales, "w1s_raw", "w1s_raw")
+        nc.sync.dma_start(out=xw_table[:].bitcast(I32), in_=x_words[0].rearrange("p n t -> p (n t)").bitcast(I32))
         nc.sync.dma_start(out=w2_raw[:].bitcast(I32), in_=w2_words[0].bitcast(I32))
         nc.sync.dma_start(nb_sb[:], nb)
-        nc.gpsimd.dma_start(out=gn_sb[:], in_=gn.rearrange("(p t) o -> p (t o)", t=PACK))
+        nc.gpsimd.dma_start(out=gn_sb[:], in_=gn.rearrange("(p t) o -> p (t o)", t=PLANES))
         nc.vector.memset(xq_scales[:].bitcast(I32), 0)
 
-        xs_picked = keep.tile([P, S], U8, name="xs_picked", tag="xs_picked")
+        xs_picked = keep.tile([P, S], U8, name="xs_picked")
         nc.vector.tensor_copy(xs_picked[:], xs_table[:].indirect(offs_sb[:]))
-        for q in range(4):
+        for q in range(QUADRANTS):
             nc.scalar.dma_start(
-                out=xq_scales[32 * q : 32 * q + 4, :].bitcast(I32),
-                in_=xs_picked[32 * q : 32 * q + 32 : 8, :].bitcast(I32),
+                out=xq_scales[QUADRANT * q : QUADRANT * q + BLOCKS, :].bitcast(I32),
+                in_=xs_picked[QUADRANT * q : QUADRANT * (q + 1) : BLOCK_PARTITIONS, :].bitcast(I32),
             )
 
-        w2s_raw = load_scale_rows([nc.sync] * 4, w2_scales, "w2s_raw", "xs_table")
-        w1 = (deal(nc.vector, w1_raw, 2, "w1_words"), deal(nc.vector, w1s_raw, 1, "w1_scales"))
-        dinv_sb = keep.tile([P, PACK, S], F32, name="dinv_sb", tag="w1_raw", align_bytes=64)
-        for t in range(PACK):
-            nc.sync.dma_start(out=dinv_sb[:, t, :], in_=dinv.rearrange("(p t) n -> p t n", t=PACK)[:, t, :])
+        w2s_raw = load_weight_scales(w2_scales, "w2s_raw", "xs_table")
+        w1 = (deal(nc.vector, w1_raw, FP4_WORD_BYTES, "w1_words"), deal(nc.vector, w1s_raw, 1, "w1_scales"))
+        dinv_sb = keep.tile([P, PLANES, S], F32, name="dinv_sb", tag="w1_raw", align_bytes=64)
+        for t in range(PLANES):
+            nc.sync.dma_start(out=dinv_sb[:, t, :], in_=dinv.rearrange("(p t) n -> p t n", t=PLANES)[:, t, :])
         xq_words = keep.tile([P, S], U32, name="xq_words", align_bytes=64)
-        half = S // 2
-        for h in range(2):
-            nc.vector.tensor_copy(
-                xq_words[:, h * half : (h + 1) * half],
-                xw_table[:].indirect(offs_sb[:, h * half // PER_COLUMN : (h + 1) * half // PER_COLUMN]),
-            )
-        w2 = (deal(nc.gpsimd, w2_raw, 2, "w2_words"), deal(nc.gpsimd, w2s_raw, 1, "w2_scales"))
-        gn_half = keep.tile([P, PACK], F32, name="gn_half")
+        for piece in (LOW, HIGH):
+            nc.vector.tensor_copy(xq_words[:, piece], xw_table[:].indirect(offs_sb[:, entries(piece)]))
+        w2 = (deal(nc.gpsimd, w2_raw, FP4_WORD_BYTES, "w2_words"), deal(nc.gpsimd, w2s_raw, 1, "w2_scales"))
+        gn_half = keep.tile([P, PLANES], F32, name="gn_half")
         nc.gpsimd.tensor_scalar(out=gn_half[:], in0=gn_sb[:], scalar1=-0.5, scalar2=None, op0=MULT)
 
-        y_sb = keep.tile([P, PACK, S], F32, name="y_sb")
+        y_sb = keep.tile([P, PLANES, S], F32, name="y_sb")
         z_codes = keep.tile([P, S], U32, name="z_codes", align_bytes=64)
         z_scales = keep.tile([P, S], U8, name="z_scales", align_bytes=64)
-        sweep1 = [psum.tile([P, S], F32, name="sweep1_%d" % t, tag="row%d" % t) for t in range(PACK)]
+        sweep1 = [psum.tile([P, S], F32, name="sweep1", tag="plane_bank%d" % t) for t in range(PLANES)]
         y_banks = []
         for c in range(CHUNKS):
-            bank = psum.tile([P, PACK, CHUNK], F32, name="y_bank", tag="bank%d" % c)
-            for t in range(PACK):
-                product(bank[:, t, :], w1, t, xq_words[:, cols(c)], xq_scales[:, cols(c)], True, True)
+            bank = psum.tile([P, PLANES, CHUNK], F32, name="y_bank", tag="chunk_bank%d" % c)
+            for t in range(PLANES):
+                product(bank[:, t, :], w1, t, xq_words[:, chunk(c)], xq_scales[:, chunk(c)], True, True)
             y_banks.append(bank)
-        z_grouped = keep.tile([P, S, PACK], BF16, name="z_grouped", align_bytes=64)
+        z_grouped = keep.tile([P, S, PLANES], BF16, name="z_grouped", tag="z_grouped", align_bytes=64)
         for c in range(CHUNKS):
             nc.vector.tensor_tensor(
-                out=z_grouped[:, cols(c), :],
+                out=z_grouped[:, chunk(c), :],
                 in0=y_banks[c][:].rearrange("p t n -> p n t"),
-                in1=gn_sb[:].unsqueeze(1).to_broadcast([P, CHUNK, PACK]),
+                in1=gn_sb[:].unsqueeze(1).to_broadcast([P, CHUNK, PLANES]),
                 op=MULT,
             )
-            nc.scalar.copy(out=y_sb[:, :, cols(c)], in_=y_banks[c][:])
-        factors = [keep.tile([P, S], F32, name="factor%d" % t) for t in range(PACK)]
-        residuals = [keep.tile([P, S], F32, name="residual%d" % t) for t in range(PACK)]
-        windows = [keep.tile([P, S], F32, name="window%d" % t) for t in range(PACK)]
-        for t in range(PACK):
-            nc.scalar.activation(out=factors[t][:], in_=dinv_sb[:, t, :], func=COPY, scale=gn_half[:, t : t + 1])
+            nc.scalar.copy(out=y_sb[:, :, chunk(c)], in_=y_banks[c][:])
 
-        def update(t, piece):
-            nc.vector.scalar_tensor_tensor(
-                out=residuals[t][:, piece], in0=sweep1[t][:, piece], scalar=-0.5, in1=y_sb[:, t, piece],
-                op0=MULT, op1=ADD,
-            )
-            nc.gpsimd.tensor_tensor(
-                out=windows[t][:, piece], in0=residuals[t][:, piece], in1=factors[t][:, piece], op=MULT
-            )
+        factors = [keep.tile([P, S], F32, name="factor%d" % t) for t in range(PLANES)]
+        residuals = [keep.tile([P, S], F32, name="residual%d" % t) for t in range(PLANES)]
+        for t in range(PLANES):
+            nc.scalar.activation(out=factors[t][:], in_=dinv_sb[:, t, :], func=COPY, scale=gn_half[:, t : t + 1])
 
         def quantize_z(piece):
             quantize(z_codes[:, piece], z_scales[:, piece], z_grouped[:, piece, :])
 
         def multiply_z(piece):
-            for t in range(PACK):
+            for t in range(PLANES):
                 product(sweep1[t][:, piece], w2, t, z_codes[:, piece], z_scales[:, piece], True, True)
 
-        low, high = slice(0, half), slice(half, S)
-        pieces = [low, cols(2), cols(3)]
-        quantize_z(low)
-        multiply_z(low)
-        update(0, low)
-        quantize_z(cols(2))
-        multiply_z(cols(2))
-        quantize_z(cols(3))
-        update(1, low)
-        multiply_z(cols(3))
-        update(0, high)
-        update(1, high)
-        update(2, slice(0, S))
-        update(3, slice(0, S))
+        def subtract(t, piece):
+            nc.vector.scalar_tensor_tensor(
+                out=residuals[t][:, piece], in0=sweep1[t][:, piece], scalar=-0.5, in1=y_sb[:, t, piece],
+                op0=MULT, op1=ADD,
+            )
 
-        def fetch(dst, t, lo, width):
-            nc.vector.tensor_copy(dst, windows[t][:].indirect(nb_sb[:, lo // PER_COLUMN : (lo + width) // PER_COLUMN]))
+        quantize_z(LOW)
+        multiply_z(LOW)
+        subtract(0, LOW)
+        quantize_z(chunk(2))
+        multiply_z(chunk(2))
+        quantize_z(chunk(3))
+        subtract(1, LOW)
+        multiply_z(chunk(3))
 
-        low_planes = keep.tile([P, 2, S], BF16, name="low_planes")
+        window_tags = ["z_grouped"] + ["window%d" % t for t in range(1, PLANES)]
+        windows = [keep.tile([P, S], F32, name="window", tag=tag, align_bytes=64) for tag in window_tags]
+
+        def scale(t, piece):
+            nc.gpsimd.tensor_tensor(
+                out=windows[t][:, piece], in0=residuals[t][:, piece], in1=factors[t][:, piece], op=MULT
+            )
+
+        scale(0, LOW)
+        subtract(0, HIGH)
+        scale(0, HIGH)
+        subtract(1, HIGH)
+        scale(1, ALL)
+        for t in range(2, PLANES):
+            subtract(t, ALL)
+            scale(t, ALL)
+
+        order = [2, 0, 1, 3]
+        kept = order[0]
+
+        def fetch(planes, t, piece):
+            nc.vector.tensor_copy(planes[:, t % 2, piece], windows[t][:].indirect(nb_sb[:, entries(piece)]))
+
+        def lay_pair(grouped, pair, planes, c):
+            nc.scalar.copy(
+                out=grouped[:, :, 2 * pair : 2 * pair + 2], in_=planes[:, :, chunk(c)].rearrange("p t n -> p n t")
+            )
+
+        planes01 = keep.tile([P, 2, S], BF16, name="planes01")
         for t in range(2):
-            for lo in range(0, S, half):
-                fetch(low_planes[:, t, lo : lo + half], t, lo, half)
-        z2_grouped = []
-        for c in range(CHUNKS):
-            grouped = keep.tile([P, CHUNK, PACK], BF16, name="z2_grouped%d" % c, tag="after%d" % c, align_bytes=64)
-            nc.scalar.copy(out=grouped[:, :, 0:2], in_=low_planes[:, :, cols(c)].rearrange("p t n -> p n t"))
-            z2_grouped.append(grouped)
-        high_planes = keep.tile([P, 2, S], BF16, name="high_planes", tag="high_planes", align_bytes=64)
-        for lo in range(0, S, half):
-            fetch(high_planes[:, 0, lo : lo + half], 2, lo, half)
-        for c in range(CHUNKS):
-            fetch(high_planes[:, 1, cols(c)], 3, c * CHUNK, CHUNK)
-            nc.scalar.copy(out=z2_grouped[c][:, :, 2:4], in_=high_planes[:, :, cols(c)].rearrange("p t n -> p n t"))
+            for piece in (LOW, HIGH):
+                fetch(planes01, t, piece)
+        z2_grouped = {}
+        for c in order:
+            z2_grouped[c] = keep.tile(
+                [P, CHUNK, PLANES], BF16, name="z2_grouped", tag="z2_grouped%d" % c, align_bytes=64
+            )
+            lay_pair(z2_grouped[c], 0, planes01, c)
+        planes23 = keep.tile([P, 2, S], BF16, name="planes23", tag="planes23", align_bytes=64)
+        for piece in (LOW, HIGH):
+            fetch(planes23, 2, piece)
+        for c in order:
+            fetch(planes23, 3, chunk(c))
+            lay_pair(z2_grouped[c], 1, planes23, c)
 
-        out_rows = out_0.rearrange("(p t) n -> p t n", t=PACK)
-        out_words = out_1[0].rearrange("p n t -> p (n t)").bitcast(I32)
-        out_codes = keep.tile([P, S], U32, name="out_codes", align_bytes=64)
-        out_scales = keep.tile([P, S], U8, name="out_scales", align_bytes=64)
-        bank_tags = [["bank0"], ["bank1"], ["bank2", "bank3"], ["row0", "row1", "row2", "row3"]]
-        banks = []
-        for c in range(CHUNKS):
+        bank_tags = [
+            ["chunk_bank0"],
+            ["chunk_bank1"],
+            ["chunk_bank2", "chunk_bank3"],
+            ["plane_bank%d" % t for t in range(PLANES)],
+        ]
+        sums = {}
+        for c, tags in zip(order, bank_tags):
             codes = keep.tile([P, CHUNK], U32, name="z2_codes%d" % c, align_bytes=64)
             scales = keep.tile([P, CHUNK], U8, name="z2_scales%d" % c, align_bytes=64)
             quantize(codes[:], scales[:], z2_grouped[c][:])
-            per_bank = PACK // len(bank_tags[c])
-            tiles = [psum.tile([P, per_bank, CHUNK], F32, name="sweep2", tag=tag) for tag in bank_tags[c]]
-            for t in range(PACK):
-                target = tiles[t // per_bank][:, t % per_bank, :]
-                if c > 0:
-                    product(target, w1, t, xq_words[:, cols(c)], xq_scales[:, cols(c)], True, False)
-                product(target, w2, t, codes[:], scales[:], c == 0, True)
-            banks.append(tiles)
+            per_bank = PLANES // len(tags)
+            sums[c] = [psum.tile([P, per_bank, CHUNK], F32, name="sweep2", tag=tag) for tag in tags]
+            for t in range(PLANES):
+                target = sums[c][t // per_bank][:, t % per_bank, :]
+                if c != kept:
+                    product(target, w1, t, xq_words[:, chunk(c)], xq_scales[:, chunk(c)], True, False)
+                product(target, w2, t, codes[:], scales[:], c == kept, True)
 
-        summed = keep.tile([P, PACK, CHUNK], F32, name="summed", tag="after2", align_bytes=64)
-        nc.vector.tensor_tensor(out=summed[:], in0=banks[0][0][:], in1=y_sb[:, :, cols(0)], op=ADD)
-        sources = [[summed]] + banks[1:]
-        order = [0, 1, 2, 3]
-        result_tags = ["after3", "high_planes", "result2", "result3"]
-        out_grouped = keep.tile([P, S, PACK], BF16, name="out_grouped", align_bytes=64)
+        summed = keep.tile([P, PLANES, CHUNK], F32, name="summed", tag="z2_grouped%d" % order[2], align_bytes=64)
+        nc.vector.tensor_tensor(out=summed[:], in0=sums[kept][0][:], in1=y_sb[:, :, chunk(kept)], op=ADD)
+        result_tags = {c: "result%d" % c for c in order}
+        result_tags[kept] = "z2_grouped%d" % order[3]
+        result_tags[order[1]] = "planes23"
+
+        out_rows = out_0.rearrange("(p t) n -> p t n", t=PLANES)
+        out_grouped = keep.tile([P, S, PLANES], BF16, name="out_grouped", align_bytes=64)
         for c in order:
-            result = keep.tile(
-                [P, PACK, CHUNK], F32, name="result%d" % c, tag=result_tags[c], align_bytes=64
-            )
-            per_bank = PACK // len(sources[c])
-            for b, source in enumerate(sources[c]):
-                rows = slice(b * per_bank, (b + 1) * per_bank)
-                engine = nc.gpsimd if c == 0 else nc.vector
-                engine.tensor_tensor(out=result[:, rows, :], in0=source[:], in1=dinv_sb[:, rows, cols(c)], op=MULT)
-            nc.sync.dma_start(out=out_rows[:, :, cols(c)], in_=result[:])
-            if c == 0:
-                nc.gpsimd.tensor_copy(out=out_grouped[:, cols(c), :], in_=result[:].rearrange("p t n -> p n t"))
+            result = keep.tile([P, PLANES, CHUNK], F32, name="result", tag=result_tags[c], align_bytes=64)
+            if c == kept:
+                nc.gpsimd.tensor_tensor(out=result[:], in0=summed[:], in1=dinv_sb[:, :, chunk(c)], op=MULT)
+                nc.gpsimd.tensor_copy(out=out_grouped[:, chunk(c), :], in_=result[:].rearrange("p t n -> p n t"))
             else:
-                interleave(out_grouped[:, cols(c), :], result[:])
-        for piece in pieces:
-            quantize(out_codes[:, piece], out_scales[:, piece], out_grouped[:, piece, :])
-        for h in (slice(0, half), slice(half, S)):
-            nc.sync.dma_start(out=out_words[:, h], in_=out_codes[:, h].bitcast(I32))
+                per_bank = PLANES // len(sums[c])
+                for b, bank in enumerate(sums[c]):
+                    rows = slice(b * per_bank, (b + 1) * per_bank)
+                    nc.vector.tensor_tensor(
+                        out=result[:, rows, :], in0=bank[:], in1=dinv_sb[:, rows, chunk(c)], op=MULT
+                    )
+                nc.scalar.copy(
+                    out=out_grouped[:, chunk(c), :].rearrange("p (g i) t -> p g t i", i=LINE),
+                    in_=result[:].rearrange("p t (g i) -> p g t i", i=LINE),
+                )
+            nc.sync.dma_start(out=out_rows[:, :, chunk(c)], in_=result[:])
 
+        out_words = out_1[0].rearrange("p n t -> p (n t)").bitcast(I32)
+        out_codes = keep.tile([P, S], U32, name="out_codes", align_bytes=64)
+        out_scales = keep.tile([P, S], U8, name="out_scales", align_bytes=64)
+        for piece in (LOW, HIGH):
+            quantize(out_codes[:, piece], out_scales[:, piece], out_grouped[:, piece, :])
+            nc.sync.dma_start(out=out_words[:, piece], in_=out_codes[:, piece].bitcast(I32))
         scale_rows = out_2[0].bitcast(I32)
-        for q in range(4):
-            queue = nc.sync if q == 0 else nc.scalar
-            queue.dma_start(out=scale_rows[4 * q : 4 * q + 4, :], in_=out_scales[32 * q : 32 * q + 4, :].bitcast(I32))
+        for q in range(QUADRANTS):
+            queue = nc.sync if q % 2 == 0 else nc.scalar
+            queue.dma_start(
+                out=scale_rows[BLOCKS * q : BLOCKS * (q + 1), :],
+                in_=out_scales[QUADRANT * q : QUADRANT * q + BLOCKS, :].bitcast(I32),
+            )

from contextlib import ExitStack

import concourse.mybir as mybir

F32 = mybir.dt.float32
BF16 = mybir.dt.bfloat16
I32 = mybir.dt.int32
U32 = mybir.dt.uint32
U16 = mybir.dt.uint16
U8 = mybir.dt.uint8
FP8X4 = mybir.dt.float8_e4m3fn_x4
FP4X4 = mybir.dt.float4_e2m1fn_x4
MULT = mybir.AluOpType.mult
ADD = mybir.AluOpType.add
COPY = mybir.ActivationFunctionType.Copy

P = 128
PLANES = 4
QUADRANTS = 4
QUADRANT = P // QUADRANTS
BLOCK_PARTITIONS = 8
BLOCKS = QUADRANT // BLOCK_PARTITIONS
T = 2048
S = 512
H = 512
CHUNK = 128
CHUNKS = S // CHUNK
HALF = S // 2
OFFSETS_PER_COLUMN = 16
WORD_BYTES = 4
FP4_WORD_BYTES = 2
LINE = 4
FLOPS = 3 * 2 * H * H * S


def chunk(c):
    return slice(c * CHUNK, (c + 1) * CHUNK)


def entries(columns):
    return slice(columns.start // OFFSETS_PER_COLUMN, columns.stop // OFFSETS_PER_COLUMN)


LOW, HIGH, ALL = slice(0, HALF), slice(HALF, S), slice(0, S)


def tile_picked_jacobi2_none_po_kernel(
    tc, x_words, x_scales, w1_words, w1_scales, gn, dinv, w2_words, w2_scales, offs, nb, out_0, out_1, out_2
):
    nc = tc.nc
    with ExitStack() as ctx:
        lists = ctx.enter_context(tc.tile_pool(name="lists", bufs=1))
        keep = ctx.enter_context(tc.tile_pool(name="keep", bufs=1))
        psum = ctx.enter_context(tc.psum_pool(name="psum", bufs=1))

        def load_weight_scales(scales, name, tag):
            raw = keep.tile([P, H], U8, name=name, tag=tag, align_bytes=64)
            rows = scales[0].bitcast(I32)
            for q in range(QUADRANTS):
                nc.sync.dma_start(
                    out=raw[QUADRANT * q : QUADRANT * (q + 1), :].bitcast(I32),
                    in_=rows[BLOCKS * q : BLOCKS * (q + 1), :]
                    .unsqueeze(0)
                    .to_broadcast([QUADRANT // BLOCKS, BLOCKS, H // WORD_BYTES]),
                )
            return raw

        def deal(engine, raw, width, name):
            dealt = keep.tile([P, width * H], U8, name=name, align_bytes=64)
            engine.tensor_copy(
                out=dealt[:].rearrange("p (t m b) -> p t m b", t=PLANES, b=width),
                in_=raw[:].rearrange("p (m t b) -> p t m b", t=PLANES, b=width),
            )
            return dealt

        def product(target, weights, t, codes, scales, start, stop):
            weight_words, weight_scales = weights
            nc.tensor.matmul_mx(
                out=target,
                lhsT=weight_words[:, FP4_WORD_BYTES * P * t : FP4_WORD_BYTES * P * (t + 1)].bitcast(FP4X4),
                lhsT_scale=weight_scales[:, P * t : P * (t + 1)],
                rhs=codes.bitcast(FP8X4),
                rhs_scale=scales,
                start=start,
                stop=stop,
            )

        def quantize(codes, scales, grouped):
            nc.vector.quantize_mx(out=codes.bitcast(FP8X4), scales=scales, in_=grouped.rearrange("p n t -> p (n t)"))

        offs_sb = lists.tile([P, S // OFFSETS_PER_COLUMN], U16, name="offs_sb")
        nb_sb = lists.tile([P, S // OFFSETS_PER_COLUMN], U16, name="nb_sb")
        xs_table = keep.tile([P, T], U8, name="xs_table", tag="xs_table", align_bytes=64)
        xw_table = keep.tile([P, T], U32, name="xw_table", align_bytes=64)
        w1_raw = keep.tile([P, FP4_WORD_BYTES * H], U8, name="w1_raw", tag="w1_raw", align_bytes=64)
        w2_raw = keep.tile([P, FP4_WORD_BYTES * H], U8, name="w2_raw", align_bytes=64)
        gn_sb = keep.tile([P, PLANES], F32, name="gn_sb")
        xq_scales = keep.tile([P, S], U8, name="xq_scales", align_bytes=64)

        nc.sync.dma_start(offs_sb[:], offs)
        nc.sync.dma_start(
            out=xs_table[:].bitcast(I32),
            in_=x_scales[0]
            .bitcast(I32)
            .unsqueeze(1)
            .to_broadcast([P // BLOCK_PARTITIONS, BLOCK_PARTITIONS, T // WORD_BYTES]),
        )
        nc.sync.dma_start(out=w1_raw[:].bitcast(I32), in_=w1_words[0].bitcast(I32))
        w1s_raw = load_weight_scales(w1_scales, "w1s_raw", "w1s_raw")
        nc.sync.dma_start(out=xw_table[:].bitcast(I32), in_=x_words[0].rearrange("p n t -> p (n t)").bitcast(I32))
        nc.sync.dma_start(out=w2_raw[:].bitcast(I32), in_=w2_words[0].bitcast(I32))
        nc.sync.dma_start(nb_sb[:], nb)
        nc.gpsimd.dma_start(out=gn_sb[:], in_=gn.rearrange("(p t) o -> p (t o)", t=PLANES))
        nc.vector.memset(xq_scales[:].bitcast(I32), 0)

        xs_picked = keep.tile([P, S], U8, name="xs_picked")
        nc.vector.tensor_copy(xs_picked[:], xs_table[:].indirect(offs_sb[:]))
        for q in range(QUADRANTS):
            nc.scalar.dma_start(
                out=xq_scales[QUADRANT * q : QUADRANT * q + BLOCKS, :].bitcast(I32),
                in_=xs_picked[QUADRANT * q : QUADRANT * (q + 1) : BLOCK_PARTITIONS, :].bitcast(I32),
            )

        w2s_raw = load_weight_scales(w2_scales, "w2s_raw", "xs_table")
        w1 = (deal(nc.vector, w1_raw, FP4_WORD_BYTES, "w1_words"), deal(nc.vector, w1s_raw, 1, "w1_scales"))
        dinv_sb = keep.tile([P, PLANES, S], F32, name="dinv_sb", tag="w1_raw", align_bytes=64)
        for t in range(PLANES):
            nc.sync.dma_start(out=dinv_sb[:, t, :], in_=dinv.rearrange("(p t) n -> p t n", t=PLANES)[:, t, :])
        xq_words = keep.tile([P, S], U32, name="xq_words", align_bytes=64)
        for piece in (LOW, HIGH):
            nc.vector.tensor_copy(xq_words[:, piece], xw_table[:].indirect(offs_sb[:, entries(piece)]))
        w2 = (deal(nc.gpsimd, w2_raw, FP4_WORD_BYTES, "w2_words"), deal(nc.gpsimd, w2s_raw, 1, "w2_scales"))
        gn_half = keep.tile([P, PLANES], F32, name="gn_half")
        nc.gpsimd.tensor_scalar(out=gn_half[:], in0=gn_sb[:], scalar1=-0.5, scalar2=None, op0=MULT)

        y_sb = keep.tile([P, PLANES, S], F32, name="y_sb")
        z_codes = keep.tile([P, S], U32, name="z_codes", align_bytes=64)
        z_scales = keep.tile([P, S], U8, name="z_scales", align_bytes=64)
        sweep1 = [psum.tile([P, S], F32, name="sweep1", tag="plane_bank%d" % t) for t in range(PLANES)]
        y_banks = []
        for c in range(CHUNKS):
            bank = psum.tile([P, PLANES, CHUNK], F32, name="y_bank", tag="chunk_bank%d" % c)
            for t in range(PLANES):
                product(bank[:, t, :], w1, t, xq_words[:, chunk(c)], xq_scales[:, chunk(c)], True, True)
            y_banks.append(bank)
        z_grouped = keep.tile([P, S, PLANES], BF16, name="z_grouped", tag="z_grouped", align_bytes=64)
        for c in range(CHUNKS):
            nc.vector.tensor_tensor(
                out=z_grouped[:, chunk(c), :],
                in0=y_banks[c][:].rearrange("p t n -> p n t"),
                in1=gn_sb[:].unsqueeze(1).to_broadcast([P, CHUNK, PLANES]),
                op=MULT,
            )
            nc.scalar.copy(out=y_sb[:, :, chunk(c)], in_=y_banks[c][:])

        factors = [keep.tile([P, S], F32, name="factor%d" % t) for t in range(PLANES)]
        residuals = [keep.tile([P, S], F32, name="residual%d" % t) for t in range(PLANES)]
        for t in range(PLANES):
            nc.scalar.activation(out=factors[t][:], in_=dinv_sb[:, t, :], func=COPY, scale=gn_half[:, t : t + 1])

        def quantize_z(piece):
            quantize(z_codes[:, piece], z_scales[:, piece], z_grouped[:, piece, :])

        def multiply_z(piece):
            for t in range(PLANES):
                product(sweep1[t][:, piece], w2, t, z_codes[:, piece], z_scales[:, piece], True, True)

        def subtract(t, piece):
            nc.vector.scalar_tensor_tensor(
                out=residuals[t][:, piece], in0=sweep1[t][:, piece], scalar=-0.5, in1=y_sb[:, t, piece],
                op0=MULT, op1=ADD,
            )

        quantize_z(LOW)
        multiply_z(LOW)
        subtract(0, LOW)
        quantize_z(chunk(2))
        multiply_z(chunk(2))
        quantize_z(chunk(3))
        subtract(1, LOW)
        multiply_z(chunk(3))

        window_tags = ["z_grouped"] + ["window%d" % t for t in range(1, PLANES)]
        windows = [keep.tile([P, S], F32, name="window", tag=tag, align_bytes=64) for tag in window_tags]

        def scale(t, piece):
            nc.gpsimd.tensor_tensor(
                out=windows[t][:, piece], in0=residuals[t][:, piece], in1=factors[t][:, piece], op=MULT
            )

        scale(0, LOW)
        subtract(0, HIGH)
        scale(0, HIGH)
        subtract(1, HIGH)
        scale(1, ALL)
        for t in range(2, PLANES):
            subtract(t, ALL)
            scale(t, ALL)

        order = [2, 0, 1, 3]
        kept = order[0]

        def fetch(planes, t, piece):
            nc.vector.tensor_copy(planes[:, t % 2, piece], windows[t][:].indirect(nb_sb[:, entries(piece)]))

        def lay_pair(grouped, pair, planes, c):
            nc.scalar.copy(
                out=grouped[:, :, 2 * pair : 2 * pair + 2], in_=planes[:, :, chunk(c)].rearrange("p t n -> p n t")
            )

        planes01 = keep.tile([P, 2, S], BF16, name="planes01")
        for t in range(2):
            for piece in (LOW, HIGH):
                fetch(planes01, t, piece)
        z2_grouped = {}
        for c in order:
            z2_grouped[c] = keep.tile(
                [P, CHUNK, PLANES], BF16, name="z2_grouped", tag="z2_grouped%d" % c, align_bytes=64
            )
            lay_pair(z2_grouped[c], 0, planes01, c)
        planes23 = keep.tile([P, 2, S], BF16, name="planes23", tag="planes23", align_bytes=64)
        for piece in (LOW, HIGH):
            fetch(planes23, 2, piece)
        for c in order:
            fetch(planes23, 3, chunk(c))
            lay_pair(z2_grouped[c], 1, planes23, c)

        bank_tags = [
            ["chunk_bank0"],
            ["chunk_bank1"],
            ["chunk_bank2", "chunk_bank3"],
            ["plane_bank%d" % t for t in range(PLANES)],
        ]
        sums = {}
        for c, tags in zip(order, bank_tags):
            codes = keep.tile([P, CHUNK], U32, name="z2_codes%d" % c, align_bytes=64)
            scales = keep.tile([P, CHUNK], U8, name="z2_scales%d" % c, align_bytes=64)
            quantize(codes[:], scales[:], z2_grouped[c][:])
            per_bank = PLANES // len(tags)
            sums[c] = [psum.tile([P, per_bank, CHUNK], F32, name="sweep2", tag=tag) for tag in tags]
            for t in range(PLANES):
                target = sums[c][t // per_bank][:, t % per_bank, :]
                if c != kept:
                    product(target, w1, t, xq_words[:, chunk(c)], xq_scales[:, chunk(c)], True, False)
                product(target, w2, t, codes[:], scales[:], c == kept, True)

        summed = keep.tile([P, PLANES, CHUNK], F32, name="summed", tag="z2_grouped%d" % order[2], align_bytes=64)
        nc.vector.tensor_tensor(out=summed[:], in0=sums[kept][0][:], in1=y_sb[:, :, chunk(kept)], op=ADD)
        result_tags = {c: "result%d" % c for c in order}
        result_tags[kept] = "z2_grouped%d" % order[3]
        result_tags[order[1]] = "planes23"

        out_rows = out_0.rearrange("(p t) n -> p t n", t=PLANES)
        out_grouped = keep.tile([P, S, PLANES], BF16, name="out_grouped", align_bytes=64)
        for c in order:
            result = keep.tile([P, PLANES, CHUNK], F32, name="result", tag=result_tags[c], align_bytes=64)
            if c == kept:
                nc.gpsimd.tensor_tensor(out=result[:], in0=summed[:], in1=dinv_sb[:, :, chunk(c)], op=MULT)
                nc.gpsimd.tensor_copy(out=out_grouped[:, chunk(c), :], in_=result[:].rearrange("p t n -> p n t"))
            else:
                per_bank = PLANES // len(sums[c])
                for b, bank in enumerate(sums[c]):
                    rows = slice(b * per_bank, (b + 1) * per_bank)
                    nc.vector.tensor_tensor(
                        out=result[:, rows, :], in0=bank[:], in1=dinv_sb[:, rows, chunk(c)], op=MULT
                    )
                nc.scalar.copy(
                    out=out_grouped[:, chunk(c), :].rearrange("p (g i) t -> p g t i", i=LINE),
                    in_=result[:].rearrange("p t (g i) -> p g t i", i=LINE),
                )
            nc.sync.dma_start(out=out_rows[:, :, chunk(c)], in_=result[:])

        out_words = out_1[0].rearrange("p n t -> p (n t)").bitcast(I32)
        out_codes = keep.tile([P, S], U32, name="out_codes", align_bytes=64)
        out_scales = keep.tile([P, S], U8, name="out_scales", align_bytes=64)
        for piece in (LOW, HIGH):
            quantize(out_codes[:, piece], out_scales[:, piece], out_grouped[:, piece, :])
            nc.sync.dma_start(out=out_words[:, piece], in_=out_codes[:, piece].bitcast(I32))
        scale_rows = out_2[0].bitcast(I32)
        for q in range(QUADRANTS):
            queue = nc.sync if q % 2 == 0 else nc.scalar
            queue.dma_start(
                out=scale_rows[BLOCKS * q : BLOCKS * (q + 1), :],
                in_=out_scales[QUADRANT * q : QUADRANT * q + BLOCKS, :].bitcast(I32),
            )
